import numpy as np
import ml_dtypes


def mxq(x, axis, fmt="e4m3"):
    dtype, down = {"e4m3": (ml_dtypes.float8_e4m3fn, 7), "e5m2": (ml_dtypes.float8_e5m2, 14)}[fmt]
    v = np.moveaxis(np.asarray(x, np.float32).astype(ml_dtypes.bfloat16).astype(np.float64), axis, -1)
    blocks = v.reshape(v.shape[:-1] + (-1, 32))
    amax = np.abs(blocks).max(-1, keepdims=True)
    byte = np.maximum(np.where(amax > 0, np.frexp(amax)[1] - 1 + 127, 0) - down, 1)
    scale = np.exp2(byte - 127.0)
    codes = (blocks / scale).astype(np.float32).astype(dtype).astype(np.float64)
    return np.moveaxis((codes * scale).reshape(v.shape), -1, axis)


WIDE = False


def mx_kscale(k):
    if not WIDE:
        return np.ones(k)
    levels = np.array([10, -10, 5, -5, 0])
    if k % 512:
        return np.exp2(np.random.permutation(np.resize(levels, k // 32))).repeat(32)
    a = np.empty((k // 512, 16))
    for p in range(k // 512):
        a[p, :8] = np.random.permutation(np.resize(levels, 8))
        for g in range(8):
            far = levels[np.abs(levels - a[p, g]) >= 10]
            a[p, g + 8] = far[np.random.randint(len(far))]
    return np.exp2(a.ravel()).repeat(32)


def f64(x):
    return np.asarray(x).astype(np.float64)


def striped(idx):
    return np.tile(idx.reshape(-1, 16).T, (8, 1)).astype(np.uint16)


def unstriped(offs):
    return offs[:16].T.reshape(-1).astype(np.int64)


def striped8(idx):
    return np.concatenate([x.reshape(-1, 16).T for x in idx]).astype(np.uint16)


def runs(offs, k):
    lists = np.stack([offs[16 * r : 16 * r + 16].T.reshape(-1) for r in range(8)]).astype(np.int64)
    return lists[np.arange(k) % 512 // 64]


def pack_weight(w):
    k, n = w.shape
    w = f64(np.asarray(w, np.float32).astype(ml_dtypes.bfloat16)).reshape(k // 32, 32, n)
    amax = np.abs(w).max(1)
    byte = np.clip(np.where(amax > 0, np.frexp(amax)[1] - 1 + 127 - 7, 1), 1, 254)
    scaled = (w * np.exp2(127.0 - byte)[:, None, :]).reshape(k, n).astype(np.float32)
    words = np.ascontiguousarray(scaled.reshape(k // 512, 128, 4, n).transpose(0, 1, 3, 2)).astype(ml_dtypes.float8_e4m3fn).view(np.uint8)
    return words, np.ascontiguousarray(byte.astype(np.uint8).reshape(k // 512, 16, n))


def unpack_weight(words, scales):
    g, p, n, _ = words.shape
    vals = np.ascontiguousarray(words).view(ml_dtypes.float8_e4m3fn).astype(np.float64) * np.repeat(np.exp2(scales.astype(np.float64) - 127.0), 8, axis=1)[..., None]
    return vals.transpose(0, 1, 3, 2).reshape(g * 512, n)


K, T, S, N, H, G, W, U = 512, 1024, 512, 512, 512, 2048, 256, 384


def setup_inputs():
    n = np.random.standard_normal
    s = mx_kscale(K)[:, None]
    u = mx_kscale(S)
    packed_xT = pack_weight(n((K, T)) * s)
    packed_dT = pack_weight(n((K, G)) / s)
    perm = np.stack([np.random.permutation(S) for _ in range(8)])
    return {
        "x_words": packed_xT[0],
        "x_scales": packed_xT[1],
        "w1": (n((K, H)) / np.sqrt(K) / s).astype(np.float32),
        "d_words": packed_dT[0],
        "d_scales": packed_dT[1],
        "gn": (np.random.uniform(0.5, 1.5, (H, 1)) * u[:, None]).astype(np.float32),
        "gk": (np.random.uniform(0.5, 1.5, (H, 1)) * u[:, None]).astype(np.float32),
        "w2": (n((H, N)) / np.sqrt(2 * H) / u[:, None]).astype(np.float32),
        "w3": (n((H, N)) / np.sqrt(2 * H) / u[:, None]).astype(np.float32),
        "offs": striped(np.random.permutation(T)[:S]),
        "kidx": striped8(np.random.randint(0, G, (8, H))),
        "two": striped(np.random.permutation(T)[:S]),
        "n1": striped(np.random.permutation(S)),
        "n2": striped(np.random.permutation(S)),
        "n3": striped8(perm[:, :W]),
        "n4": striped8(perm[:, W:]),
        "n5": striped(np.random.permutation(S)[:U]),
        "n6": striped(np.random.permutation(S)[:U]),
    }


def reference(x_words, x_scales, w1, d_words, d_scales, gn, gk, w2, w3, offs, kidx, two, n1, n2, n3, n4, n5, n6):
    xq = unpack_weight(x_words, x_scales)[:, unstriped(offs)]
    y = mxq(f64(w1), 0, "e4m3").T @ xq
    z = f64(gn) * (y * (y[:, unstriped(n1)] - y[:, unstriped(n2)]))
    d_kidx = unpack_weight(d_words, d_scales)[np.arange(K)[:, None], runs(kidx, K)]
    x_two = unpack_weight(x_words, x_scales)[:, unstriped(two)]
    s = 0.0625 * (d_kidx.T @ x_two)
    pa = s[np.arange(H)[:, None], runs(n3, H)]
    pb = s[np.arange(H)[:, None], runs(n4, H)]
    rb = np.maximum(0.5 * pa, pb)
    ra = pb - pa
    ds = np.zeros((H, S))
    ds[np.arange(H)[:, None], runs(n3, H)] = ra
    dt = ds.copy()
    dt[np.arange(H)[:, None], runs(n4, H)] = rb
    z2 = f64(gk) * dt
    h = mxq(f64(w2), 0, "e4m3").T @ mxq(z, 0, "e4m3") + mxq(f64(w3), 0, "e4m3").T @ mxq(z2, 0, "e4m3")
    pa2 = h[:, unstriped(n6)]
    old = h[:, unstriped(n5)]
    ra2 = np.minimum(pa2, old) - (0.5 * pa2)
    out = h.copy()
    out[:, unstriped(n5)] = ra2
    return out

@@ -1,0 +1,242 @@
+from contextlib import ExitStack
+
+import concourse.mybir as mybir
+
+F32 = mybir.dt.float32
+BF16 = mybir.dt.bfloat16
+I32 = mybir.dt.int32
+U32 = mybir.dt.uint32
+U16 = mybir.dt.uint16
+U8 = mybir.dt.uint8
+FP8X4 = mybir.dt.float8_e4m3fn_x4
+ALU = mybir.AluOpType
+COPY = mybir.ActivationFunctionType.Copy
+
+P = 128
+PACK = 4
+K, T, S, N, H, G, W, U = 512, 1024, 512, 512, 512, 2048, 256, 384
+FLOPS = 4 * 2 * 512 * 512 * 512
+
+
+def tile_picked_jkeywindliftkmin_none_p_kernel(
+    tc, x_words, x_scales, w1, d_words, d_scales, gn, gk, w2, w3, offs, kidx, two, n1, n2, n3, n4, n5, n6, out
+):
+    nc = tc.nc
+    with ExitStack() as ctx:
+        keep = ctx.enter_context(tc.tile_pool(name="keep", bufs=1))
+        work = ctx.enter_context(tc.tile_pool(name="work", bufs=4))
+        psum = ctx.enter_context(tc.psum_pool(name="psum", bufs=1))
+
+        def load_list(src, name):
+            lst = keep.tile([P, src.shape[1]], U16, name=name)
+            nc.sync.dma_start(lst[:], src)
+            return lst
+
+        def words_of(src):
+            return src[0].rearrange("p n t -> p (n t)").bitcast(I32)
+
+        d_bytes = keep.tile([P, G], U8, name="d_bytes")
+        x_bytes = keep.tile([P, T], U8, name="x_bytes")
+        key_plane = keep.tile([P, H], U8, name="key_plane", align_bytes=64)
+        nc.vector.memset(d_bytes[:].bitcast(I32), 0)
+        nc.gpsimd.memset(x_bytes[:].bitcast(I32), 0)
+        nc.gpsimd.memset(key_plane[:].bitcast(I32), 0)
+
+        def load_rows(src, name, cols, tag):
+            raw = keep.tile([P, PACK, cols.stop - cols.start], F32, name=name, tag=tag)
+            nc.sync.dma_start(raw[:], src.rearrange("(p j) c -> p j c", j=PACK)[:, :, cols])
+            return raw
+
+        halves = (slice(0, 256), slice(256, 512))
+        nc.scalar.dma_start(d_bytes[0:P:8, :].bitcast(I32), d_scales[0].bitcast(I32))
+        for q in range(4):
+            nc.scalar.dma_start(x_bytes[32 * q : 32 * q + 4, :].bitcast(I32), x_scales[0, 4 * q : 4 * q + 4, :].bitcast(I32))
+        kidx_l = load_list(kidx, "kidx_l")
+        two_l = load_list(two, "two_l")
+        offs_l = load_list(offs, "offs_l")
+        n3_l = load_list(n3, "n3_l")
+        n4_l = load_list(n4, "n4_l")
+        x_tab = keep.tile([P, T], U32, name="x_tab")
+        nc.sync.dma_start(x_tab[:].bitcast(I32), words_of(x_words))
+        d_tab = keep.tile([P, G], U32, name="d_tab")
+        nc.sync.dma_start(d_tab[:].bitcast(I32), words_of(d_words))
+        n1_l = load_list(n1, "n1_l")
+        w1_raw = [load_rows(w1, f"w1_raw{half}", halves[half], f"raw{half}") for half in range(2)]
+        n2_l = load_list(n2, "n2_l")
+        n5_l = load_list(n5, "n5_l")
+        n6_l = load_list(n6, "n6_l")
+        gn_sb = keep.tile([P, PACK], F32, name="gn_sb")
+        nc.gpsimd.dma_start(gn_sb[:], gn.rearrange("(p t) o -> p (t o)", t=PACK))
+        gk_sb = keep.tile([P, PACK], F32, name="gk_sb")
+        nc.gpsimd.dma_start(gk_sb[:], gk.rearrange("(p t) o -> p (t o)", t=PACK))
+
+        two_words = keep.tile([P, S], U32, name="two_words", align_bytes=64)
+        nc.vector.tensor_copy(two_words[:], x_tab[:].indirect(two_l[:]))
+        key_bytes = keep.tile([P, H], U8, name="key_bytes")
+        nc.vector.tensor_copy(key_bytes[:], d_bytes[:].indirect(kidx_l[:]))
+        key_bytes_dealt = keep.tile([P, H], U8, name="key_bytes_dealt")
+        nc.vector.tensor_copy(
+            key_bytes_dealt[:].rearrange("p (t m) -> p t m", t=PACK), key_bytes[:].rearrange("p (m t) -> p t m", t=PACK)
+        )
+        for j in range(4):
+            nc.scalar.dma_start(key_plane[j:P:32, :].bitcast(I32), key_bytes_dealt[8 * j : P : 32, :].bitcast(I32))
+
+        key_words = keep.tile([P, H], U32, name="key_words")
+        nc.vector.tensor_copy(key_words[:], d_tab[:].indirect(kidx_l[:]))
+        key_dealt = keep.tile([P, H], U32, name="key_dealt", align_bytes=64)
+        nc.vector.tensor_copy(
+            key_dealt[:].bitcast(I32).rearrange("p (t m) -> p m t", t=PACK),
+            key_words[:].bitcast(I32).rearrange("p (m t) -> p m t", t=PACK),
+        )
+        two_bytes = keep.tile([P, S], U8, name="two_bytes", align_bytes=64)
+        nc.vector.tensor_copy(two_bytes[:], x_bytes[:].indirect(two_l[:]))
+
+        def product(bank, lhs, rhs, t, start, stop):
+            cols = slice(t * P, (t + 1) * P)
+            nc.tensor.matmul_mx(
+                out=bank[:],
+                lhsT=lhs[0][:, cols].bitcast(FP8X4),
+                lhsT_scale=lhs[1][:, cols],
+                rhs=rhs[0][:].bitcast(FP8X4),
+                rhs_scale=rhs[1][:],
+                start=start,
+                stop=stop,
+            )
+
+        s_banks = [psum.tile([P, S], F32, name=f"s_bank{t}", tag=f"sh{t}") for t in range(PACK)]
+        for t in range(PACK):
+            product(s_banks[t], (key_dealt, key_plane), (two_words, two_bytes), t, True, True)
+
+        tok_bytes = keep.tile([P, S], U8, name="tok_bytes", align_bytes=64)
+        nc.vector.tensor_copy(tok_bytes[:], x_bytes[:].indirect(offs_l[:]))
+        tok_words = keep.tile([P, S], U32, name="tok_words", align_bytes=64)
+        nc.vector.tensor_copy(tok_words[:], x_tab[:].indirect(offs_l[:]))
+
+        def quantize(grouped, name):
+            cols = grouped.shape[1] // PACK
+            codes = keep.tile([P, cols], U32, name=name + "_codes", align_bytes=64)
+            plane = keep.tile([P, cols], U8, name=name + "_plane", align_bytes=64)
+            nc.vector.quantize_mx(out=codes[:].bitcast(FP8X4), scales=plane[:], in_=grouped)
+            return codes, plane
+
+        w1_grp = keep.tile([P, H * PACK], BF16, name="w1_grp", align_bytes=64)
+        w1_view = w1_grp[:].rearrange("p (t m j) -> p m j t", t=PACK, j=PACK)
+        for half in range(2):
+            nc.scalar.activation(
+                w1_view[:, half * (P // 2) : (half + 1) * (P // 2)],
+                w1_raw[half][:].rearrange("p j (m t) -> p m j t", t=PACK),
+                COPY,
+            )
+        w1_codes, w1_plane = quantize(w1_grp[:], "w1")
+
+        w3_raw = load_rows(w3, "w3_raw", slice(0, N), "raw0")
+        w2_raw = load_rows(w2, "w2_raw", slice(0, N), "raw1")
+
+        y_banks = [psum.tile([P, S], F32, name=f"y_bank{t}") for t in range(PACK)]
+        for t in range(PACK):
+            product(y_banks[t], (w1_codes, w1_plane), (tok_words, tok_bytes), t, True, True)
+
+        def interleave(copy, grouped, planes):
+            copy(
+                grouped.rearrange("p (c i t) -> p c t i", i=4, t=PACK),
+                planes.rearrange("p t (c i) -> p c t i", i=4),
+            )
+
+        z_planes = keep.tile([P, PACK, S], BF16, name="z_planes")
+        z2_planes = keep.tile([P, PACK, S], BF16, name="z2_planes")
+
+        def y_fetch(t):
+            y_win = work.tile([P, S], F32, name="y_win")
+            nc.scalar.copy(y_win[:], y_banks[t][:])
+            at1 = work.tile([P, S], F32, name="at1")
+            at2 = work.tile([P, S], F32, name="at2")
+            for dst, lst in ((at1, n1_l), (at2, n2_l)):
+                for half in range(2):
+                    nc.scalar.activation(dst[:, half * W : (half + 1) * W], y_win[:].indirect(lst[:, half * 16 : (half + 1) * 16]), COPY)
+            return at1, at2
+
+        def y_finish(t, at1, at2):
+            diff = work.tile([P, S], F32, name="diff")
+            nc.vector.tensor_tensor(diff[:], at1[:], at2[:], ALU.subtract)
+            nc.vector.scalar_tensor_tensor(z_planes[:, t, :], diff[:], gn_sb[:, t : t + 1], y_banks[t][:], ALU.mult, ALU.mult)
+
+        def s_fetch(t):
+            s_win = work.tile([P, S], F32, name="s_win")
+            nc.scalar.activation(s_win[:], s_banks[t][:], COPY, scale=0.0625)
+            neg_pa = work.tile([P, W], F32, name="neg_pa")
+            pb = work.tile([P, W], F32, name="pb")
+            nc.scalar.activation(neg_pa[:], s_win[:].indirect(n3_l[:]), COPY, scale=-1.0)
+            nc.scalar.activation(pb[:], s_win[:].indirect(n4_l[:]), COPY)
+            return neg_pa, pb
+
+        def s_finish(t, neg_pa, pb):
+            rb = work.tile([P, W], F32, name="rb")
+            nc.vector.scalar_tensor_tensor(rb[:], neg_pa[:], -0.5, pb[:], ALU.mult, ALU.max)
+            dt = work.tile([P, S], F32, name="dt")
+            nc.vector.tensor_tensor(dt[:].indirect(n3_l[:]), pb[:], neg_pa[:], ALU.add)
+            nc.vector.tensor_copy(dt[:].indirect(n4_l[:]), rb[:])
+            nc.vector.tensor_scalar(z2_planes[:, t, :], dt[:], gk_sb[:, t : t + 1], None, ALU.mult)
+
+        w_grp = {}
+
+        def w_group(name, raw):
+            grp = keep.tile([P, N * PACK], BF16, name=name + "_grp", align_bytes=64)
+            for c in range(4):
+                interleave(nc.scalar.copy, grp[:, c * N : (c + 1) * N], raw[:, :, c * P : (c + 1) * P])
+            w_grp[name] = grp
+
+        s_finish(0, *s_fetch(0))
+        for t in range(PACK):
+            if t + 1 < PACK:
+                s_finish(t + 1, *s_fetch(t + 1))
+            y_finish(t, *y_fetch(t))
+        w_group("w3", w3_raw)
+        z2_grp = keep.tile([P, S * PACK], BF16, name="z2_grp", align_bytes=64)
+        interleave(nc.scalar.copy, z2_grp[:], z2_planes[:])
+        w_group("w2", w2_raw)
+
+        z_grp = keep.tile([P, S * PACK], BF16, name="z_grp", align_bytes=64)
+        interleave(nc.vector.tensor_copy, z_grp[:], z_planes[:])
+        w3_q = quantize(w_grp["w3"][:], "w3")
+        z_q = quantize(z_grp[:], "z")
+        z2_q = quantize(z2_grp[:], "z2")
+        w2_q = quantize(w_grp["w2"][:], "w2")
+
+        h_banks = [psum.tile([P, S], F32, name=f"h_bank{t}", tag=f"sh{t}") for t in range(4)]
+        for t in range(4):
+            product(h_banks[t], w3_q, z2_q, t, True, False)
+            product(h_banks[t], w2_q, z_q, t, False, True)
+
+        h_win, neg_half, old = [], [], {}
+        for t in range(4):
+            win = keep.tile([P, S], F32, name=f"h_win{t}")
+            if t == 1:
+                nc.vector.tensor_copy(win[:], h_banks[t][:])
+            else:
+                nc.scalar.copy(win[:], h_banks[t][:])
+            half = keep.tile([P, U], F32, name=f"neg_half{t}")
+            nc.scalar.activation(half[:], win[:].indirect(n6_l[:]), COPY, scale=-0.5)
+            got = keep.tile([P, U], F32, name=f"old{t}")
+            new = keep.tile([P, U], F32, name=f"new{t}")
+            if t % 2 == 0:
+                nc.vector.tensor_tensor(got[:], win[:].indirect(n5_l[:]), half[:], ALU.add)
+                nc.vector.scalar_tensor_tensor(new[:], half[:], -1.0, got[:], ALU.mult, ALU.min)
+            else:
+                if t == 1:
+                    nc.vector.tensor_copy(got[:], win[:].indirect(n5_l[:]))
+                else:
+                    nc.scalar.activation(got[:], win[:].indirect(n5_l[:]), COPY)
+                nc.vector.scalar_tensor_tensor(new[:], half[:], -2.0, got[:], ALU.mult, ALU.min)
+            h_win.append(win)
+            neg_half.append(half)
+            old[t] = new
+        for t in range(4):
+            if t % 2 == 0:
+                nc.scalar.activation(h_win[t][:].indirect(n5_l[:]), old[t][:], COPY)
+            else:
+                for part in range(2):
+                    cols = slice(part * (U // 2), (part + 1) * (U // 2))
+                    nc.vector.tensor_tensor(
+                        h_win[t][:].indirect(n5_l[:, part * 12 : (part + 1) * 12]), old[t][:, cols], neg_half[t][:, cols], ALU.add
+                    )
+            nc.sync.dma_start(out[t * P : (t + 1) * P, :], h_win[t][:])

@@ -15,6 +15,7 @@ COPY = mybir.ActivationFunctionType.Copy
 P = 128
 PACK = 4
 K, T, S, N, H, G, W, U = 512, 1024, 512, 512, 512, 2048, 256, 384
+SPARE = 8
 FLOPS = 4 * 2 * 512 * 512 * 512
 
 
@@ -38,40 +39,34 @@ def tile_picked_jkeywindliftkmin_none_p_kernel(
         d_bytes = keep.tile([P, G], U8, name="d_bytes")
         x_bytes = keep.tile([P, T], U8, name="x_bytes")
         key_plane = keep.tile([P, H], U8, name="key_plane", align_bytes=64)
-        nc.vector.memset(d_bytes[:].bitcast(I32), 0)
-        nc.gpsimd.memset(x_bytes[:].bitcast(I32), 0)
-        nc.gpsimd.memset(key_plane[:].bitcast(I32), 0)
+        nc.gpsimd.memset(d_bytes[:].bitcast(I32), 0)
+        nc.vector.memset(x_bytes[:].bitcast(I32), 0)
+        zeros = keep.tile([P, SPARE], F32, name="zeros", tag="w1_stage")
+        nc.vector.memset(zeros[:], 0.0)
+        nc.vector.memset(key_plane[:].bitcast(I32), 0)
 
-        def load_rows(src, name, cols, tag):
-            raw = keep.tile([P, PACK, cols.stop - cols.start], F32, name=name, tag=tag)
-            nc.sync.dma_start(raw[:], src.rearrange("(p j) c -> p j c", j=PACK)[:, :, cols])
+        def load_rows(src, name):
+            raw = keep.tile([P, PACK, N], F32, name=name)
+            nc.sync.dma_start(raw[:], src.rearrange("(p j) c -> p j c", j=PACK))
             return raw
 
         halves = (slice(0, 256), slice(256, 512))
-        nc.scalar.dma_start(d_bytes[0:P:8, :].bitcast(I32), d_scales[0].bitcast(I32))
         for q in range(4):
             nc.scalar.dma_start(x_bytes[32 * q : 32 * q + 4, :].bitcast(I32), x_scales[0, 4 * q : 4 * q + 4, :].bitcast(I32))
+        y_wins = [keep.tile([P, S + SPARE], F32, name=f"y_win{t}") for t in range(PACK)]
+        for win in y_wins:
+            nc.scalar.activation(win[:, S:], zeros[:], COPY)
         kidx_l = load_list(kidx, "kidx_l")
         two_l = load_list(two, "two_l")
-        offs_l = load_list(offs, "offs_l")
-        n3_l = load_list(n3, "n3_l")
-        n4_l = load_list(n4, "n4_l")
-        x_tab = keep.tile([P, T], U32, name="x_tab")
-        nc.sync.dma_start(x_tab[:].bitcast(I32), words_of(x_words))
+        nc.sync.dma_start(d_bytes[0:P:8, :].bitcast(I32), d_scales[0].bitcast(I32))
         d_tab = keep.tile([P, G], U32, name="d_tab")
         nc.sync.dma_start(d_tab[:].bitcast(I32), words_of(d_words))
-        n1_l = load_list(n1, "n1_l")
-        w1_raw = [load_rows(w1, f"w1_raw{half}", halves[half], f"raw{half}") for half in range(2)]
-        n2_l = load_list(n2, "n2_l")
-        n5_l = load_list(n5, "n5_l")
-        n6_l = load_list(n6, "n6_l")
-        gn_sb = keep.tile([P, PACK], F32, name="gn_sb")
-        nc.gpsimd.dma_start(gn_sb[:], gn.rearrange("(p t) o -> p (t o)", t=PACK))
-        gk_sb = keep.tile([P, PACK], F32, name="gk_sb")
-        nc.gpsimd.dma_start(gk_sb[:], gk.rearrange("(p t) o -> p (t o)", t=PACK))
+        x_tab = keep.tile([P, T], U32, name="x_tab")
+        nc.sync.dma_start(x_tab[:].bitcast(I32), words_of(x_words))
+        w1_raw = keep.tile([P, 2, PACK, H // 2], F32, name="w1_raw", tag="w1_stage")
+        for half in range(2):
+            nc.scalar.dma_start(w1_raw[:, half], w1.rearrange("(p j) c -> p j c", j=PACK)[:, :, halves[half]])
 
-        two_words = keep.tile([P, S], U32, name="two_words", align_bytes=64)
-        nc.vector.tensor_copy(two_words[:], x_tab[:].indirect(two_l[:]))
         key_bytes = keep.tile([P, H], U8, name="key_bytes")
         nc.vector.tensor_copy(key_bytes[:], d_bytes[:].indirect(kidx_l[:]))
         key_bytes_dealt = keep.tile([P, H], U8, name="key_bytes_dealt")
@@ -79,17 +74,33 @@ def tile_picked_jkeywindliftkmin_none_p_kernel(
             key_bytes_dealt[:].rearrange("p (t m) -> p t m", t=PACK), key_bytes[:].rearrange("p (m t) -> p t m", t=PACK)
         )
         for j in range(4):
-            nc.scalar.dma_start(key_plane[j:P:32, :].bitcast(I32), key_bytes_dealt[8 * j : P : 32, :].bitcast(I32))
+            nc.sync.dma_start(key_plane[j:P:32, :].bitcast(I32), key_bytes_dealt[8 * j : P : 32, :].bitcast(I32))
+
+        offs_l = load_list(offs, "offs_l")
+        n3_l = load_list(n3, "n3_l")
+        n4_l = load_list(n4, "n4_l")
+        gn_sb = keep.tile([P, PACK], F32, name="gn_sb")
+        nc.sync.dma_start(gn_sb[:], gn.rearrange("(p t) o -> p (t o)", t=PACK))
+        n1_l = load_list(n1, "n1_l")
+        n2_l = load_list(n2, "n2_l")
+        gk_sb = keep.tile([P, PACK], F32, name="gk_sb")
+        nc.sync.dma_start(gk_sb[:], gk.rearrange("(p t) o -> p (t o)", t=PACK))
+        w2_raw = load_rows(w2, "w2_raw")
+        w3_raw = load_rows(w3, "w3_raw")
+        n5_l = load_list(n5, "n5_l")
+        n6_l = load_list(n6, "n6_l")
 
         key_words = keep.tile([P, H], U32, name="key_words")
         nc.vector.tensor_copy(key_words[:], d_tab[:].indirect(kidx_l[:]))
+        two_bytes = keep.tile([P, S], U8, name="two_bytes", align_bytes=64)
+        nc.vector.tensor_copy(two_bytes[:], x_bytes[:].indirect(two_l[:]))
         key_dealt = keep.tile([P, H], U32, name="key_dealt", align_bytes=64)
         nc.vector.tensor_copy(
             key_dealt[:].bitcast(I32).rearrange("p (t m) -> p m t", t=PACK),
             key_words[:].bitcast(I32).rearrange("p (m t) -> p m t", t=PACK),
         )
-        two_bytes = keep.tile([P, S], U8, name="two_bytes", align_bytes=64)
-        nc.vector.tensor_copy(two_bytes[:], x_bytes[:].indirect(two_l[:]))
+        two_words = keep.tile([P, S], U32, name="two_words", align_bytes=64)
+        nc.vector.tensor_copy(two_words[:], x_tab[:].indirect(two_l[:]))
 
         def product(bank, lhs, rhs, t, start, stop):
             cols = slice(t * P, (t + 1) * P)
@@ -124,17 +135,23 @@ def tile_picked_jkeywindliftkmin_none_p_kernel(
         for half in range(2):
             nc.scalar.activation(
                 w1_view[:, half * (P // 2) : (half + 1) * (P // 2)],
-                w1_raw[half][:].rearrange("p j (m t) -> p m j t", t=PACK),
+                w1_raw[:, half].rearrange("p j (m t) -> p m j t", t=PACK),
                 COPY,
             )
         w1_codes, w1_plane = quantize(w1_grp[:], "w1")
 
-        w3_raw = load_rows(w3, "w3_raw", slice(0, N), "raw0")
-        w2_raw = load_rows(w2, "w2_raw", slice(0, N), "raw1")
-
-        y_banks = [psum.tile([P, S], F32, name=f"y_bank{t}") for t in range(PACK)]
-        for t in range(PACK):
-            product(y_banks[t], (w1_codes, w1_plane), (tok_words, tok_bytes), t, True, True)
+        y_banks = [psum.tile([P, PACK, P], F32, name=f"y_bank{c}") for c in range(4)]
+        for c in range(4):
+            for t in range(PACK):
+                nc.tensor.matmul_mx(
+                    out=y_banks[c][:, t, :],
+                    lhsT=w1_codes[:, t * P : (t + 1) * P].bitcast(FP8X4),
+                    lhsT_scale=w1_plane[:, t * P : (t + 1) * P],
+                    rhs=tok_words[:, c * P : (c + 1) * P].bitcast(FP8X4),
+                    rhs_scale=tok_bytes[:, c * P : (c + 1) * P],
+                    start=True,
+                    stop=True,
+                )
 
         def interleave(copy, grouped, planes):
             copy(
@@ -142,23 +159,28 @@ def tile_picked_jkeywindliftkmin_none_p_kernel(
                 planes.rearrange("p t (c i) -> p c t i", i=4),
             )
 
-        z_planes = keep.tile([P, PACK, S], BF16, name="z_planes")
+        diff = keep.tile([P, PACK, S], F32, name="diff")
         z2_planes = keep.tile([P, PACK, S], BF16, name="z2_planes")
 
         def y_fetch(t):
-            y_win = work.tile([P, S], F32, name="y_win")
-            nc.scalar.copy(y_win[:], y_banks[t][:])
+            for c in range(4):
+                nc.scalar.activation(y_wins[t][:, c * P : (c + 1) * P], y_banks[c][:, t, :], COPY, scale=gn_sb[:, t : t + 1])
             at1 = work.tile([P, S], F32, name="at1")
             at2 = work.tile([P, S], F32, name="at2")
-            for dst, lst in ((at1, n1_l), (at2, n2_l)):
-                for half in range(2):
-                    nc.scalar.activation(dst[:, half * W : (half + 1) * W], y_win[:].indirect(lst[:, half * 16 : (half + 1) * 16]), COPY)
+            nc.scalar.activation(at1[:], y_wins[t][:].indirect(n1_l[:]), COPY)
+            nc.scalar.activation(at2[:], y_wins[t][:].indirect(n2_l[:]), COPY)
             return at1, at2
 
         def y_finish(t, at1, at2):
-            diff = work.tile([P, S], F32, name="diff")
-            nc.vector.tensor_tensor(diff[:], at1[:], at2[:], ALU.subtract)
-            nc.vector.scalar_tensor_tensor(z_planes[:, t, :], diff[:], gn_sb[:, t : t + 1], y_banks[t][:], ALU.mult, ALU.mult)
+            nc.vector.tensor_tensor(diff[:, t, :], at1[:], at2[:], ALU.subtract)
+
+        def z_round(c):
+            nc.vector.tensor_tensor(
+                z_grp[:, c * S : (c + 1) * S].rearrange("p (c i t) -> p c t i", i=2, t=PACK),
+                diff[:, :, c * P : (c + 1) * P].rearrange("p t (c i) -> p c t i", i=2),
+                y_banks[c][:].rearrange("p t (c i) -> p c t i", i=2),
+                ALU.mult,
+            )
 
         def s_fetch(t):
             s_win = work.tile([P, S], F32, name="s_win")
@@ -171,72 +193,107 @@ def tile_picked_jkeywindliftkmin_none_p_kernel(
 
         def s_finish(t, neg_pa, pb):
             rb = work.tile([P, W], F32, name="rb")
-            nc.vector.scalar_tensor_tensor(rb[:], neg_pa[:], -0.5, pb[:], ALU.mult, ALU.max)
             dt = work.tile([P, S], F32, name="dt")
             nc.vector.tensor_tensor(dt[:].indirect(n3_l[:]), pb[:], neg_pa[:], ALU.add)
+            nc.vector.scalar_tensor_tensor(rb[:], neg_pa[:], -0.5, pb[:], ALU.mult, ALU.max)
             nc.vector.tensor_copy(dt[:].indirect(n4_l[:]), rb[:])
-            nc.vector.tensor_scalar(z2_planes[:, t, :], dt[:], gk_sb[:, t : t + 1], None, ALU.mult)
+            return dt
 
-        w_grp = {}
+        def z2_round(t, dt, on_vector):
+            if on_vector:
+                nc.vector.tensor_scalar(z2_planes[:, t, :], dt[:], gk_sb[:, t : t + 1], None, ALU.mult)
+            else:
+                nc.scalar.activation(z2_planes[:, t, :], dt[:], COPY, scale=gk_sb[:, t : t + 1])
 
-        def w_group(name, raw):
-            grp = keep.tile([P, N * PACK], BF16, name=name + "_grp", align_bytes=64)
-            for c in range(4):
-                interleave(nc.scalar.copy, grp[:, c * N : (c + 1) * N], raw[:, :, c * P : (c + 1) * P])
-            w_grp[name] = grp
+        w2_grp = keep.tile([P, N * PACK], BF16, name="w2_grp", align_bytes=64)
+        w3_grp = keep.tile([P, N * PACK], BF16, name="w3_grp", align_bytes=64)
 
-        s_finish(0, *s_fetch(0))
-        for t in range(PACK):
-            if t + 1 < PACK:
-                s_finish(t + 1, *s_fetch(t + 1))
-            y_finish(t, *y_fetch(t))
-        w_group("w3", w3_raw)
-        z2_grp = keep.tile([P, S * PACK], BF16, name="z2_grp", align_bytes=64)
-        interleave(nc.scalar.copy, z2_grp[:], z2_planes[:])
-        w_group("w2", w2_raw)
+        def w_group(copy, grp, raw, chunks):
+            for c in chunks:
+                interleave(copy, grp[:, c * N : (c + 1) * N], raw[:, :, c * P : (c + 1) * P])
 
         z_grp = keep.tile([P, S * PACK], BF16, name="z_grp", align_bytes=64)
-        interleave(nc.vector.tensor_copy, z_grp[:], z_planes[:])
-        w3_q = quantize(w_grp["w3"][:], "w3")
+        z2_grp = keep.tile([P, S * PACK], BF16, name="z2_grp", align_bytes=64)
+        dts = [s_finish(0, *s_fetch(0))]
+        for t in range(PACK):
+            if t + 1 < PACK:
+                dts.append(s_finish(t + 1, *s_fetch(t + 1)))
+            y_finish(t, *y_fetch(t))
+        for c in range(4):
+            z_round(c)
         z_q = quantize(z_grp[:], "z")
+        w_group(nc.scalar.copy, w2_grp, w2_raw, range(4))
+        w2_q = quantize(w2_grp[:], "w2")
+        for t in range(PACK):
+            z2_round(t, dts[t], False)
+        interleave(nc.vector.tensor_copy, z2_grp[:], z2_planes[:])
+        w_group(nc.scalar.copy, w3_grp, w3_raw, range(4))
+        w3_q = [quantize(w3_grp[:, :N], "w3_0")]
         z2_q = quantize(z2_grp[:], "z2")
-        w2_q = quantize(w_grp["w2"][:], "w2")
+        w3_q.extend(quantize(w3_grp[:, t * N : (t + 1) * N], f"w3_{t}") for t in range(1, 4))
 
         h_banks = [psum.tile([P, S], F32, name=f"h_bank{t}", tag=f"sh{t}") for t in range(4)]
         for t in range(4):
-            product(h_banks[t], w3_q, z2_q, t, True, False)
-            product(h_banks[t], w2_q, z_q, t, False, True)
+            product(h_banks[t], w2_q, z_q, t, True, False)
+            product(h_banks[t], w3_q[t], z2_q, 0, False, True)
 
-        h_win, neg_half, old = [], [], {}
-        for t in range(4):
-            win = keep.tile([P, S], F32, name=f"h_win{t}")
-            if t == 1:
-                nc.vector.tensor_copy(win[:], h_banks[t][:])
-            else:
-                nc.scalar.copy(win[:], h_banks[t][:])
-            half = keep.tile([P, U], F32, name=f"neg_half{t}")
-            nc.scalar.activation(half[:], win[:].indirect(n6_l[:]), COPY, scale=-0.5)
-            got = keep.tile([P, U], F32, name=f"old{t}")
-            new = keep.tile([P, U], F32, name=f"new{t}")
-            if t % 2 == 0:
-                nc.vector.tensor_tensor(got[:], win[:].indirect(n5_l[:]), half[:], ALU.add)
-                nc.vector.scalar_tensor_tensor(new[:], half[:], -1.0, got[:], ALU.mult, ALU.min)
-            else:
-                if t == 1:
-                    nc.vector.tensor_copy(got[:], win[:].indirect(n5_l[:]))
-                else:
-                    nc.scalar.activation(got[:], win[:].indirect(n5_l[:]), COPY)
-                nc.vector.scalar_tensor_tensor(new[:], half[:], -2.0, got[:], ALU.mult, ALU.min)
-            h_win.append(win)
-            neg_half.append(half)
-            old[t] = new
-        for t in range(4):
-            if t % 2 == 0:
-                nc.scalar.activation(h_win[t][:].indirect(n5_l[:]), old[t][:], COPY)
-            else:
-                for part in range(2):
-                    cols = slice(part * (U // 2), (part + 1) * (U // 2))
-                    nc.vector.tensor_tensor(
-                        h_win[t][:].indirect(n5_l[:, part * 12 : (part + 1) * 12]), old[t][:, cols], neg_half[t][:, cols], ALU.add
-                    )
+        h_win = [keep.tile([P, S], F32, name=f"h_win{t}") for t in range(4)]
+        neg_half = [keep.tile([P, U], F32, name=f"neg_half{t}") for t in range(4)]
+        old = [keep.tile([P, U], F32, name=f"old{t}") for t in range(4)]
+        new = [keep.tile([P, U], F32, name=f"new{t}") for t in range(4)]
+
+        def h_out(t, copy):
+            copy(h_win[t][:], h_banks[t][:])
+
+        def h_half(t):
+            nc.scalar.activation(neg_half[t][:], h_win[t][:].indirect(n6_l[:]), COPY, scale=-0.5)
+
+        def h_whole(t):
+            nc.vector.tensor_tensor(old[t][:], h_win[t][:].indirect(n5_l[:]), neg_half[t][:], ALU.add)
+            nc.vector.scalar_tensor_tensor(new[t][:], neg_half[t][:], -1.0, old[t][:], ALU.mult, ALU.min)
+
+        def h_old_s(t):
+            nc.scalar.activation(old[t][:], h_win[t][:].indirect(n5_l[:]), COPY)
+
+        def h_old_v(t):
+            nc.vector.tensor_copy(old[t][:], h_win[t][:].indirect(n5_l[:]))
+
+        def h_min(t):
+            nc.vector.scalar_tensor_tensor(new[t][:], neg_half[t][:], -2.0, old[t][:], ALU.mult, ALU.min)
+
+        def put_s(t):
+            nc.scalar.activation(h_win[t][:].indirect(n5_l[:]), new[t][:], COPY)
+
+        def put_v(t, part):
+            cols = slice(part * (U // 2), (part + 1) * (U // 2))
+            nc.vector.tensor_tensor(
+                h_win[t][:].indirect(n5_l[:, part * 12 : (part + 1) * 12]), new[t][:, cols], neg_half[t][:, cols], ALU.add
+            )
+
+        def store(t):
             nc.sync.dma_start(out[t * P : (t + 1) * P, :], h_win[t][:])
+
+        h_out(0, nc.scalar.copy)
+        h_out(1, nc.vector.tensor_copy)
+        h_out(2, nc.vector.tensor_copy)
+        h_half(0)
+        h_old_v(1)
+        h_whole(0)
+        h_half(1)
+        h_min(1)
+        h_half(2)
+        h_out(3, nc.scalar.copy)
+        put_v(1, 0)
+        h_whole(2)
+        put_v(1, 1)
+        store(1)
+        h_half(3)
+        h_old_s(3)
+        h_min(3)
+        put_s(0)
+        store(0)
+        put_s(2)
+        store(2)
+        put_v(3, 0)
+        put_v(3, 1)
+        store(3)

@@ -25,7 +25,6 @@ def tile_picked_jkeywindliftkmin_none_p_kernel(
     nc = tc.nc
     with ExitStack() as ctx:
         keep = ctx.enter_context(tc.tile_pool(name="keep", bufs=1))
-        work = ctx.enter_context(tc.tile_pool(name="work", bufs=4))
         psum = ctx.enter_context(tc.psum_pool(name="psum", bufs=1))
 
         def load_list(src, name):
@@ -41,8 +40,6 @@ def tile_picked_jkeywindliftkmin_none_p_kernel(
         key_plane = keep.tile([P, H], U8, name="key_plane", align_bytes=64)
         nc.gpsimd.memset(d_bytes[:].bitcast(I32), 0)
         nc.vector.memset(x_bytes[:].bitcast(I32), 0)
-        zeros = keep.tile([P, SPARE], F32, name="zeros", tag="w1_stage")
-        nc.vector.memset(zeros[:], 0.0)
         nc.vector.memset(key_plane[:].bitcast(I32), 0)
 
         def load_rows(src, name):
@@ -55,17 +52,19 @@ def tile_picked_jkeywindliftkmin_none_p_kernel(
             nc.scalar.dma_start(x_bytes[32 * q : 32 * q + 4, :].bitcast(I32), x_scales[0, 4 * q : 4 * q + 4, :].bitcast(I32))
         y_wins = [keep.tile([P, S + SPARE], F32, name=f"y_win{t}") for t in range(PACK)]
         for win in y_wins:
-            nc.scalar.activation(win[:, S:], zeros[:], COPY)
+            nc.gpsimd.memset(win[:, S:], 0.0)
         kidx_l = load_list(kidx, "kidx_l")
         two_l = load_list(two, "two_l")
         nc.sync.dma_start(d_bytes[0:P:8, :].bitcast(I32), d_scales[0].bitcast(I32))
-        d_tab = keep.tile([P, G], U32, name="d_tab")
-        nc.sync.dma_start(d_tab[:].bitcast(I32), words_of(d_words))
         x_tab = keep.tile([P, T], U32, name="x_tab")
         nc.sync.dma_start(x_tab[:].bitcast(I32), words_of(x_words))
-        w1_raw = keep.tile([P, 2, PACK, H // 2], F32, name="w1_raw", tag="w1_stage")
-        for half in range(2):
-            nc.scalar.dma_start(w1_raw[:, half], w1.rearrange("(p j) c -> p j c", j=PACK)[:, :, halves[half]])
+        d_tab = keep.tile([P, G], U32, name="d_tab")
+        nc.sync.dma_start(d_tab[:].bitcast(I32), words_of(d_words))
+        w1_raw = keep.tile([P, 2, PACK, H // 2], F32, name="w1_raw")
+        w1_rows = w1.rearrange("(p j) c -> p j c", j=PACK)
+        nc.sync.dma_start(w1_raw[:, 0], w1_rows[:, :, halves[0]])
+        offs_l = load_list(offs, "offs_l")
+        nc.sync.dma_start(w1_raw[:, 1], w1_rows[:, :, halves[1]])
 
         key_bytes = keep.tile([P, H], U8, name="key_bytes")
         nc.vector.tensor_copy(key_bytes[:], d_bytes[:].indirect(kidx_l[:]))
@@ -74,9 +73,9 @@ def tile_picked_jkeywindliftkmin_none_p_kernel(
             key_bytes_dealt[:].rearrange("p (t m) -> p t m", t=PACK), key_bytes[:].rearrange("p (m t) -> p t m", t=PACK)
         )
         for j in range(4):
-            nc.sync.dma_start(key_plane[j:P:32, :].bitcast(I32), key_bytes_dealt[8 * j : P : 32, :].bitcast(I32))
+            queue = nc.sync if j == 3 else nc.scalar
+            queue.dma_start(key_plane[j:P:32, :].bitcast(I32), key_bytes_dealt[8 * j : P : 32, :].bitcast(I32))
 
-        offs_l = load_list(offs, "offs_l")
         n3_l = load_list(n3, "n3_l")
         n4_l = load_list(n4, "n4_l")
         gn_sb = keep.tile([P, PACK], F32, name="gn_sb")
@@ -90,17 +89,17 @@ def tile_picked_jkeywindliftkmin_none_p_kernel(
         n5_l = load_list(n5, "n5_l")
         n6_l = load_list(n6, "n6_l")
 
-        key_words = keep.tile([P, H], U32, name="key_words")
-        nc.vector.tensor_copy(key_words[:], d_tab[:].indirect(kidx_l[:]))
+        two_words = keep.tile([P, S], U32, name="two_words", align_bytes=64)
+        nc.vector.tensor_copy(two_words[:], x_tab[:].indirect(two_l[:]))
         two_bytes = keep.tile([P, S], U8, name="two_bytes", align_bytes=64)
         nc.vector.tensor_copy(two_bytes[:], x_bytes[:].indirect(two_l[:]))
+        key_words = keep.tile([P, H], U32, name="key_words")
+        nc.vector.tensor_copy(key_words[:], d_tab[:].indirect(kidx_l[:]))
         key_dealt = keep.tile([P, H], U32, name="key_dealt", align_bytes=64)
         nc.vector.tensor_copy(
             key_dealt[:].bitcast(I32).rearrange("p (t m) -> p m t", t=PACK),
             key_words[:].bitcast(I32).rearrange("p (m t) -> p m t", t=PACK),
         )
-        two_words = keep.tile([P, S], U32, name="two_words", align_bytes=64)
-        nc.vector.tensor_copy(two_words[:], x_tab[:].indirect(two_l[:]))
 
         def product(bank, lhs, rhs, t, start, stop):
             cols = slice(t * P, (t + 1) * P)
@@ -162,17 +161,21 @@ def tile_picked_jkeywindliftkmin_none_p_kernel(
         diff = keep.tile([P, PACK, S], F32, name="diff")
         z2_planes = keep.tile([P, PACK, S], BF16, name="z2_planes")
 
-        def y_fetch(t):
+        at1 = [keep.tile([P, S], F32, name=f"at1_{t}") for t in range(PACK)]
+        at2 = [keep.tile([P, S], F32, name=f"at2_{t}") for t in range(PACK)]
+
+        def y_out(t):
             for c in range(4):
                 nc.scalar.activation(y_wins[t][:, c * P : (c + 1) * P], y_banks[c][:, t, :], COPY, scale=gn_sb[:, t : t + 1])
-            at1 = work.tile([P, S], F32, name="at1")
-            at2 = work.tile([P, S], F32, name="at2")
-            nc.scalar.activation(at1[:], y_wins[t][:].indirect(n1_l[:]), COPY)
-            nc.scalar.activation(at2[:], y_wins[t][:].indirect(n2_l[:]), COPY)
-            return at1, at2
 
-        def y_finish(t, at1, at2):
-            nc.vector.tensor_tensor(diff[:, t, :], at1[:], at2[:], ALU.subtract)
+        def y_at1(t):
+            nc.scalar.activation(at1[t][:], y_wins[t][:].indirect(n1_l[:]), COPY)
+
+        def y_at2(t, half):
+            nc.scalar.activation(at2[t][:, halves[half]], y_wins[t][:].indirect(n2_l[:, half * 16 : (half + 1) * 16]), COPY)
+
+        def y_diff(t):
+            nc.vector.tensor_tensor(diff[:, t, :], at1[t][:], at2[t][:], ALU.subtract)
 
         def z_round(c):
             nc.vector.tensor_tensor(
@@ -182,22 +185,25 @@ def tile_picked_jkeywindliftkmin_none_p_kernel(
                 ALU.mult,
             )
 
-        def s_fetch(t):
-            s_win = work.tile([P, S], F32, name="s_win")
-            nc.scalar.activation(s_win[:], s_banks[t][:], COPY, scale=0.0625)
-            neg_pa = work.tile([P, W], F32, name="neg_pa")
-            pb = work.tile([P, W], F32, name="pb")
-            nc.scalar.activation(neg_pa[:], s_win[:].indirect(n3_l[:]), COPY, scale=-1.0)
-            nc.scalar.activation(pb[:], s_win[:].indirect(n4_l[:]), COPY)
-            return neg_pa, pb
+        s_wins = [keep.tile([P, S], F32, name=f"s_win{t}") for t in range(PACK)]
+        neg_pa = [keep.tile([P, W], F32, name=f"neg_pa{t}") for t in range(PACK)]
+        pb = [keep.tile([P, W], F32, name=f"pb{t}") for t in range(PACK)]
+        rb = [keep.tile([P, W], F32, name=f"rb{t}") for t in range(PACK)]
+        dts = [keep.tile([P, S], F32, name=f"dt{t}") for t in range(PACK)]
 
-        def s_finish(t, neg_pa, pb):
-            rb = work.tile([P, W], F32, name="rb")
-            dt = work.tile([P, S], F32, name="dt")
-            nc.vector.tensor_tensor(dt[:].indirect(n3_l[:]), pb[:], neg_pa[:], ALU.add)
-            nc.vector.scalar_tensor_tensor(rb[:], neg_pa[:], -0.5, pb[:], ALU.mult, ALU.max)
-            nc.vector.tensor_copy(dt[:].indirect(n4_l[:]), rb[:])
-            return dt
+        def s_out(t):
+            nc.scalar.activation(s_wins[t][:], s_banks[t][:], COPY, scale=0.0625)
+
+        def s_pair(t):
+            nc.scalar.activation(neg_pa[t][:], s_wins[t][:].indirect(n3_l[:]), COPY, scale=-1.0)
+            nc.scalar.activation(pb[t][:], s_wins[t][:].indirect(n4_l[:]), COPY)
+
+        def put_ra(t):
+            nc.vector.tensor_tensor(dts[t][:].indirect(n3_l[:]), pb[t][:], neg_pa[t][:], ALU.add)
+            nc.vector.scalar_tensor_tensor(rb[t][:], neg_pa[t][:], -0.5, pb[t][:], ALU.mult, ALU.max)
+
+        def put_rb(t):
+            nc.vector.tensor_copy(dts[t][:].indirect(n4_l[:]), rb[t][:])
 
         def z2_round(t, dt, on_vector):
             if on_vector:
@@ -214,27 +220,67 @@ def tile_picked_jkeywindliftkmin_none_p_kernel(
 
         z_grp = keep.tile([P, S * PACK], BF16, name="z_grp", align_bytes=64)
         z2_grp = keep.tile([P, S * PACK], BF16, name="z2_grp", align_bytes=64)
-        dts = [s_finish(0, *s_fetch(0))]
-        for t in range(PACK):
-            if t + 1 < PACK:
-                dts.append(s_finish(t + 1, *s_fetch(t + 1)))
-            y_finish(t, *y_fetch(t))
+        s_out(0)
+        s_pair(0)
+        put_ra(0)
+        s_out(1)
+        s_pair(1)
+        put_ra(1)
+        put_rb(0)
+        put_rb(1)
+        z2_round(0, dts[0], True)
+        s_out(2)
+        y_out(0)
+        y_out(1)
+        y_at1(0)
+        y_at2(0, 0)
+        s_pair(2)
+        put_ra(2)
+        z2_round(1, dts[1], True)
+        y_at2(0, 1)
+        y_diff(0)
+        put_rb(2)
+        s_out(3)
+        y_at1(1)
+        y_out(2)
+        y_at2(1, 0)
+        s_pair(3)
+        put_ra(3)
+        y_at2(1, 1)
+        y_diff(1)
+        put_rb(3)
+        y_out(3)
+        y_at1(2)
+        y_at2(2, 0)
+        y_at2(2, 1)
+        y_diff(2)
+        y_at1(3)
+        y_at2(3, 0)
+        y_at2(3, 1)
+        y_diff(3)
+        def w_tile(t):
+            quantized = []
+            for grp, raw, name in ((w2_grp, w2_raw, "w2"), (w3_grp, w3_raw, "w3")):
+                w_group(nc.scalar.copy, grp, raw, (t,))
+                quantized.append(quantize(grp[:, t * N : (t + 1) * N], f"{name}_{t}"))
+            return quantized
+
         for c in range(4):
             z_round(c)
         z_q = quantize(z_grp[:], "z")
-        w_group(nc.scalar.copy, w2_grp, w2_raw, range(4))
-        w2_q = quantize(w2_grp[:], "w2")
-        for t in range(PACK):
+        for t in (2, 3):
             z2_round(t, dts[t], False)
-        interleave(nc.vector.tensor_copy, z2_grp[:], z2_planes[:])
-        w_group(nc.scalar.copy, w3_grp, w3_raw, range(4))
-        w3_q = [quantize(w3_grp[:, :N], "w3_0")]
+        w_q = [w_tile(0)]
+        interleave(nc.scalar.copy, z2_grp[:, 256 * PACK :], z2_planes[:, :, 256:])
+        interleave(nc.vector.tensor_copy, z2_grp[:, : 256 * PACK], z2_planes[:, :, :256])
         z2_q = quantize(z2_grp[:], "z2")
-        w3_q.extend(quantize(w3_grp[:, t * N : (t + 1) * N], f"w3_{t}") for t in range(1, 4))
+        w_q.extend(w_tile(t) for t in range(1, 4))
+        w2_q = [pair[0] for pair in w_q]
+        w3_q = [pair[1] for pair in w_q]
 
         h_banks = [psum.tile([P, S], F32, name=f"h_bank{t}", tag=f"sh{t}") for t in range(4)]
         for t in range(4):
-            product(h_banks[t], w2_q, z_q, t, True, False)
+            product(h_banks[t], w2_q[t], z_q, 0, True, False)
             product(h_banks[t], w3_q[t], z2_q, 0, False, True)
 
         h_win = [keep.tile([P, S], F32, name=f"h_win{t}") for t in range(4)]

@@ -40,6 +40,8 @@ def tile_picked_jkeywindliftkmin_none_p_kernel(
         key_plane = keep.tile([P, H], U8, name="key_plane", align_bytes=64)
         nc.gpsimd.memset(d_bytes[:].bitcast(I32), 0)
         nc.vector.memset(x_bytes[:].bitcast(I32), 0)
+        zeros = keep.tile([P, SPARE], F32, name="zeros")
+        nc.vector.memset(zeros[:], 0.0)
         nc.vector.memset(key_plane[:].bitcast(I32), 0)
 
         def load_rows(src, name):
@@ -52,19 +54,19 @@ def tile_picked_jkeywindliftkmin_none_p_kernel(
             nc.scalar.dma_start(x_bytes[32 * q : 32 * q + 4, :].bitcast(I32), x_scales[0, 4 * q : 4 * q + 4, :].bitcast(I32))
         y_wins = [keep.tile([P, S + SPARE], F32, name=f"y_win{t}") for t in range(PACK)]
         for win in y_wins:
-            nc.gpsimd.memset(win[:, S:], 0.0)
+            nc.scalar.activation(win[:, S:], zeros[:], COPY)
         kidx_l = load_list(kidx, "kidx_l")
         two_l = load_list(two, "two_l")
         nc.sync.dma_start(d_bytes[0:P:8, :].bitcast(I32), d_scales[0].bitcast(I32))
+        w1_raw = keep.tile([P, 2, PACK, H // 2], F32, name="w1_raw")
+        w1_rows = w1.rearrange("(p j) c -> p j c", j=PACK)
+        nc.sync.dma_start(w1_raw[:, 0], w1_rows[:, :, halves[0]])
         x_tab = keep.tile([P, T], U32, name="x_tab")
         nc.sync.dma_start(x_tab[:].bitcast(I32), words_of(x_words))
         d_tab = keep.tile([P, G], U32, name="d_tab")
         nc.sync.dma_start(d_tab[:].bitcast(I32), words_of(d_words))
-        w1_raw = keep.tile([P, 2, PACK, H // 2], F32, name="w1_raw")
-        w1_rows = w1.rearrange("(p j) c -> p j c", j=PACK)
-        nc.sync.dma_start(w1_raw[:, 0], w1_rows[:, :, halves[0]])
-        offs_l = load_list(offs, "offs_l")
         nc.sync.dma_start(w1_raw[:, 1], w1_rows[:, :, halves[1]])
+        offs_l = load_list(offs, "offs_l")
 
         key_bytes = keep.tile([P, H], U8, name="key_bytes")
         nc.vector.tensor_copy(key_bytes[:], d_bytes[:].indirect(kidx_l[:]))
@@ -130,18 +132,18 @@ def tile_picked_jkeywindliftkmin_none_p_kernel(
             return codes, plane
 
         w1_grp = keep.tile([P, H * PACK], BF16, name="w1_grp", align_bytes=64)
-        w1_view = w1_grp[:].rearrange("p (t m j) -> p m j t", t=PACK, j=PACK)
+        w1_view = w1_grp[:].rearrange("p (t m j) -> p m t j", t=PACK, j=PACK)
         for half in range(2):
             nc.scalar.activation(
                 w1_view[:, half * (P // 2) : (half + 1) * (P // 2)],
-                w1_raw[:, half].rearrange("p j (m t) -> p m j t", t=PACK),
+                w1_raw[:, half].rearrange("p j (m t) -> p m t j", t=PACK),
                 COPY,
             )
         w1_codes, w1_plane = quantize(w1_grp[:], "w1")
 
         y_banks = [psum.tile([P, PACK, P], F32, name=f"y_bank{c}") for c in range(4)]
-        for c in range(4):
-            for t in range(PACK):
+        for t in range(PACK):
+            for c in range(4):
                 nc.tensor.matmul_mx(
                     out=y_banks[c][:, t, :],
                     lhsT=w1_codes[:, t * P : (t + 1) * P].bitcast(FP8X4),

@@ -14,8 +14,12 @@ COPY = mybir.ActivationFunctionType.Copy
 
 P = 128
 PACK = 4
-K, T, S, N, H, G, W, U = 512, 1024, 512, 512, 512, 2048, 256, 384
+T, G = 1024, 2048
+S, H, N = 512, 512, 512
+W, U = 256, 384
+PER_COL = 16
 SPARE = 8
+Z2_ON_VECTOR = 128
 FLOPS = 4 * 2 * 512 * 512 * 512
 
 
@@ -26,103 +30,41 @@ def tile_picked_jkeywindliftkmin_none_p_kernel(
     with ExitStack() as ctx:
         keep = ctx.enter_context(tc.tile_pool(name="keep", bufs=1))
         psum = ctx.enter_context(tc.psum_pool(name="psum", bufs=1))
+        halves = (slice(0, 256), slice(256, 512))
 
         def load_list(src, name):
             lst = keep.tile([P, src.shape[1]], U16, name=name)
             nc.sync.dma_start(lst[:], src)
             return lst
 
-        def words_of(src):
-            return src[0].rearrange("p n t -> p (n t)").bitcast(I32)
+        def load_words(src, name):
+            table = keep.tile([P, src.shape[2]], U32, name=name)
+            nc.sync.dma_start(table[:].bitcast(I32), src[0].rearrange("p n t -> p (n t)").bitcast(I32))
+            return table
 
-        d_bytes = keep.tile([P, G], U8, name="d_bytes")
-        x_bytes = keep.tile([P, T], U8, name="x_bytes")
-        key_plane = keep.tile([P, H], U8, name="key_plane", align_bytes=64)
-        nc.gpsimd.memset(d_bytes[:].bitcast(I32), 0)
-        nc.vector.memset(x_bytes[:].bitcast(I32), 0)
-        zeros = keep.tile([P, SPARE], F32, name="zeros")
-        nc.vector.memset(zeros[:], 0.0)
-        nc.vector.memset(key_plane[:].bitcast(I32), 0)
+        def load_gain(src, name):
+            gain = keep.tile([P, PACK], F32, name=name)
+            nc.sync.dma_start(gain[:], src.rearrange("(p t) o -> p (t o)", t=PACK))
+            return gain
 
-        def load_rows(src, name):
+        def k_rows(weight):
+            return weight.rearrange("(p j) c -> p j c", j=PACK)
+
+        def load_weight(src, name):
             raw = keep.tile([P, PACK, N], F32, name=name)
-            nc.sync.dma_start(raw[:], src.rearrange("(p j) c -> p j c", j=PACK))
+            nc.sync.dma_start(raw[:], k_rows(src))
             return raw
 
-        halves = (slice(0, 256), slice(256, 512))
-        for q in range(4):
-            nc.scalar.dma_start(x_bytes[32 * q : 32 * q + 4, :].bitcast(I32), x_scales[0, 4 * q : 4 * q + 4, :].bitcast(I32))
-        y_wins = [keep.tile([P, S + SPARE], F32, name=f"y_win{t}") for t in range(PACK)]
-        for win in y_wins:
-            nc.scalar.activation(win[:, S:], zeros[:], COPY)
-        kidx_l = load_list(kidx, "kidx_l")
-        two_l = load_list(two, "two_l")
-        nc.sync.dma_start(d_bytes[0:P:8, :].bitcast(I32), d_scales[0].bitcast(I32))
-        w1_raw = keep.tile([P, 2, PACK, H // 2], F32, name="w1_raw")
-        w1_rows = w1.rearrange("(p j) c -> p j c", j=PACK)
-        nc.sync.dma_start(w1_raw[:, 0], w1_rows[:, :, halves[0]])
-        x_tab = keep.tile([P, T], U32, name="x_tab")
-        nc.sync.dma_start(x_tab[:].bitcast(I32), words_of(x_words))
-        d_tab = keep.tile([P, G], U32, name="d_tab")
-        nc.sync.dma_start(d_tab[:].bitcast(I32), words_of(d_words))
-        nc.sync.dma_start(w1_raw[:, 1], w1_rows[:, :, halves[1]])
-        offs_l = load_list(offs, "offs_l")
+        def gather(table, lst, dtype, name):
+            picked = keep.tile([P, S], dtype, name=name, align_bytes=64)
+            nc.vector.tensor_copy(picked[:], table[:].indirect(lst[:]))
+            return picked
 
-        key_bytes = keep.tile([P, H], U8, name="key_bytes")
-        nc.vector.tensor_copy(key_bytes[:], d_bytes[:].indirect(kidx_l[:]))
-        key_bytes_dealt = keep.tile([P, H], U8, name="key_bytes_dealt")
-        nc.vector.tensor_copy(
-            key_bytes_dealt[:].rearrange("p (t m) -> p t m", t=PACK), key_bytes[:].rearrange("p (m t) -> p t m", t=PACK)
-        )
-        for j in range(4):
-            queue = nc.sync if j == 3 else nc.scalar
-            queue.dma_start(key_plane[j:P:32, :].bitcast(I32), key_bytes_dealt[8 * j : P : 32, :].bitcast(I32))
-
-        n3_l = load_list(n3, "n3_l")
-        n4_l = load_list(n4, "n4_l")
-        gn_sb = keep.tile([P, PACK], F32, name="gn_sb")
-        nc.sync.dma_start(gn_sb[:], gn.rearrange("(p t) o -> p (t o)", t=PACK))
-        n1_l = load_list(n1, "n1_l")
-        n2_l = load_list(n2, "n2_l")
-        gk_sb = keep.tile([P, PACK], F32, name="gk_sb")
-        nc.sync.dma_start(gk_sb[:], gk.rearrange("(p t) o -> p (t o)", t=PACK))
-        w2_raw = load_rows(w2, "w2_raw")
-        w3_raw = load_rows(w3, "w3_raw")
-        n5_l = load_list(n5, "n5_l")
-        n6_l = load_list(n6, "n6_l")
-
-        two_words = keep.tile([P, S], U32, name="two_words", align_bytes=64)
-        nc.vector.tensor_copy(two_words[:], x_tab[:].indirect(two_l[:]))
-        two_bytes = keep.tile([P, S], U8, name="two_bytes", align_bytes=64)
-        nc.vector.tensor_copy(two_bytes[:], x_bytes[:].indirect(two_l[:]))
-        key_words = keep.tile([P, H], U32, name="key_words")
-        nc.vector.tensor_copy(key_words[:], d_tab[:].indirect(kidx_l[:]))
-        key_dealt = keep.tile([P, H], U32, name="key_dealt", align_bytes=64)
-        nc.vector.tensor_copy(
-            key_dealt[:].bitcast(I32).rearrange("p (t m) -> p m t", t=PACK),
-            key_words[:].bitcast(I32).rearrange("p (m t) -> p m t", t=PACK),
-        )
-
-        def product(bank, lhs, rhs, t, start, stop):
-            cols = slice(t * P, (t + 1) * P)
-            nc.tensor.matmul_mx(
-                out=bank[:],
-                lhsT=lhs[0][:, cols].bitcast(FP8X4),
-                lhsT_scale=lhs[1][:, cols],
-                rhs=rhs[0][:].bitcast(FP8X4),
-                rhs_scale=rhs[1][:],
-                start=start,
-                stop=stop,
+        def interleave(copy, grouped, rows):
+            copy(
+                grouped.rearrange("p (c i t) -> p c t i", i=4, t=PACK),
+                rows.rearrange("p t (c i) -> p c t i", i=4),
             )
-
-        s_banks = [psum.tile([P, S], F32, name=f"s_bank{t}", tag=f"sh{t}") for t in range(PACK)]
-        for t in range(PACK):
-            product(s_banks[t], (key_dealt, key_plane), (two_words, two_bytes), t, True, True)
-
-        tok_bytes = keep.tile([P, S], U8, name="tok_bytes", align_bytes=64)
-        nc.vector.tensor_copy(tok_bytes[:], x_bytes[:].indirect(offs_l[:]))
-        tok_words = keep.tile([P, S], U32, name="tok_words", align_bytes=64)
-        nc.vector.tensor_copy(tok_words[:], x_tab[:].indirect(offs_l[:]))
 
         def quantize(grouped, name):
             cols = grouped.shape[1] // PACK
@@ -131,217 +73,242 @@ def tile_picked_jkeywindliftkmin_none_p_kernel(
             nc.vector.quantize_mx(out=codes[:].bitcast(FP8X4), scales=plane[:], in_=grouped)
             return codes, plane
 
+        def product(dst, lhs, lhs_cols, rhs, rhs_cols, start, stop):
+            nc.tensor.matmul_mx(
+                out=dst,
+                lhsT=lhs[0][:, lhs_cols].bitcast(FP8X4),
+                lhsT_scale=lhs[1][:, lhs_cols],
+                rhs=rhs[0][:, rhs_cols].bitcast(FP8X4),
+                rhs_scale=rhs[1][:, rhs_cols],
+                start=start,
+                stop=stop,
+            )
+
+        def block(i):
+            return slice(i * P, (i + 1) * P)
+
+        whole = slice(0, S)
+
+        d_bytes = keep.tile([P, G], U8, name="d_bytes")
+        x_bytes = keep.tile([P, T], U8, name="x_bytes")
+        key_plane = keep.tile([P, H], U8, name="key_plane", align_bytes=64)
+        zeros = keep.tile([P, SPARE], F32, name="zeros")
+        nc.gpsimd.memset(d_bytes[:].bitcast(I32), 0)
+        nc.vector.memset(x_bytes[:].bitcast(I32), 0)
+        nc.vector.memset(zeros[:], 0.0)
+        nc.vector.memset(key_plane[:].bitcast(I32), 0)
+
+        for q in range(4):
+            nc.scalar.dma_start(
+                x_bytes[32 * q : 32 * q + 4, :].bitcast(I32), x_scales[0, 4 * q : 4 * q + 4, :].bitcast(I32)
+            )
+        y_win = [keep.tile([P, S + SPARE], F32, name=f"y_win{t}") for t in range(PACK)]
+        for win in y_win:
+            nc.scalar.activation(win[:, S:], zeros[:], COPY)
+        kidx_l = load_list(kidx, "kidx_l")
+        two_l = load_list(two, "two_l")
+        nc.sync.dma_start(d_bytes[0:P:8, :].bitcast(I32), d_scales[0].bitcast(I32))
+        w1_raw = keep.tile([P, 2, PACK, H // 2], F32, name="w1_raw")
+        nc.sync.dma_start(w1_raw[:, 0], k_rows(w1)[:, :, halves[0]])
+        x_tab = load_words(x_words, "x_tab")
+        d_tab = load_words(d_words, "d_tab")
+        nc.sync.dma_start(w1_raw[:, 1], k_rows(w1)[:, :, halves[1]])
+        offs_l = load_list(offs, "offs_l")
+
+        key_bytes = gather(d_bytes, kidx_l, U8, "key_bytes")
+        key_bytes_dealt = keep.tile([P, H], U8, name="key_bytes_dealt")
+        nc.vector.tensor_copy(
+            key_bytes_dealt[:].rearrange("p (t m) -> p t m", t=PACK),
+            key_bytes[:].rearrange("p (m t) -> p t m", t=PACK),
+        )
+        for j, queue in enumerate((nc.scalar, nc.scalar, nc.scalar, nc.sync)):
+            queue.dma_start(key_plane[j:P:32, :].bitcast(I32), key_bytes_dealt[8 * j : P : 32, :].bitcast(I32))
+
+        n3_l = load_list(n3, "n3_l")
+        n4_l = load_list(n4, "n4_l")
+        gn_sb = load_gain(gn, "gn_sb")
+        n1_l = load_list(n1, "n1_l")
+        n2_l = load_list(n2, "n2_l")
+        gk_sb = load_gain(gk, "gk_sb")
+        w2_raw = load_weight(w2, "w2_raw")
+        w3_raw = load_weight(w3, "w3_raw")
+        n5_l = load_list(n5, "n5_l")
+        n6_l = load_list(n6, "n6_l")
+
+        two_q = (gather(x_tab, two_l, U32, "two_words"), gather(x_bytes, two_l, U8, "two_bytes"))
+        key_words = gather(d_tab, kidx_l, U32, "key_words")
+        key_dealt = keep.tile([P, H], U32, name="key_dealt", align_bytes=64)
+        nc.vector.tensor_copy(
+            key_dealt[:].bitcast(I32).rearrange("p (t m) -> p m t", t=PACK),
+            key_words[:].bitcast(I32).rearrange("p (m t) -> p m t", t=PACK),
+        )
+        s_bank = [psum.tile([P, S], F32, name=f"s_bank{t}", tag=f"s_or_h{t}") for t in range(PACK)]
+        for t in range(PACK):
+            product(s_bank[t][:], (key_dealt, key_plane), block(t), two_q, whole, True, True)
+
+        tok_bytes = gather(x_bytes, offs_l, U8, "tok_bytes")
+        tok_words = gather(x_tab, offs_l, U32, "tok_words")
         w1_grp = keep.tile([P, H * PACK], BF16, name="w1_grp", align_bytes=64)
-        w1_view = w1_grp[:].rearrange("p (t m j) -> p m t j", t=PACK, j=PACK)
+        w1_dealt = w1_grp[:].rearrange("p (t m j) -> p m t j", t=PACK, j=PACK)
         for half in range(2):
             nc.scalar.activation(
-                w1_view[:, half * (P // 2) : (half + 1) * (P // 2)],
+                w1_dealt[:, half * (P // 2) : (half + 1) * (P // 2)],
                 w1_raw[:, half].rearrange("p j (m t) -> p m t j", t=PACK),
                 COPY,
             )
-        w1_codes, w1_plane = quantize(w1_grp[:], "w1")
-
-        y_banks = [psum.tile([P, PACK, P], F32, name=f"y_bank{c}") for c in range(4)]
+        w1_q = quantize(w1_grp[:], "w1")
+        y_bank = [psum.tile([P, PACK, P], F32, name=f"y_bank{c}") for c in range(S // P)]
         for t in range(PACK):
-            for c in range(4):
-                nc.tensor.matmul_mx(
-                    out=y_banks[c][:, t, :],
-                    lhsT=w1_codes[:, t * P : (t + 1) * P].bitcast(FP8X4),
-                    lhsT_scale=w1_plane[:, t * P : (t + 1) * P],
-                    rhs=tok_words[:, c * P : (c + 1) * P].bitcast(FP8X4),
-                    rhs_scale=tok_bytes[:, c * P : (c + 1) * P],
-                    start=True,
-                    stop=True,
-                )
+            for c in range(S // P):
+                product(y_bank[c][:, t, :], w1_q, block(t), (tok_words, tok_bytes), block(c), True, True)
 
-        def interleave(copy, grouped, planes):
-            copy(
-                grouped.rearrange("p (c i t) -> p c t i", i=4, t=PACK),
-                planes.rearrange("p t (c i) -> p c t i", i=4),
-            )
+        s_win = [keep.tile([P, S], F32, name=f"s_win{t}") for t in range(PACK)]
+        neg_pa = [keep.tile([P, W], F32, name=f"neg_pa{t}") for t in range(PACK)]
+        pb = [keep.tile([P, W], F32, name=f"pb{t}") for t in range(PACK)]
+        rb = [keep.tile([P, W], F32, name=f"rb{t}") for t in range(PACK)]
+        dt = [keep.tile([P, S], F32, name=f"dt{t}") for t in range(PACK)]
+        z2_rows = keep.tile([P, PACK, S], BF16, name="z2_rows")
 
-        diff = keep.tile([P, PACK, S], F32, name="diff")
-        z2_planes = keep.tile([P, PACK, S], BF16, name="z2_planes")
+        def s_out(t):
+            nc.scalar.activation(s_win[t][:], s_bank[t][:], COPY, scale=0.0625)
+
+        def s_pairs(t):
+            nc.scalar.activation(neg_pa[t][:], s_win[t][:].indirect(n3_l[:]), COPY, scale=-1.0)
+            nc.scalar.activation(pb[t][:], s_win[t][:].indirect(n4_l[:]), COPY)
+
+        def put_ra_make_rb(t):
+            nc.vector.tensor_tensor(dt[t][:].indirect(n3_l[:]), pb[t][:], neg_pa[t][:], ALU.add)
+            nc.vector.scalar_tensor_tensor(rb[t][:], neg_pa[t][:], -0.5, pb[t][:], ALU.mult, ALU.max)
+
+        def put_rb(t):
+            nc.vector.tensor_copy(dt[t][:].indirect(n4_l[:]), rb[t][:])
 
         at1 = [keep.tile([P, S], F32, name=f"at1_{t}") for t in range(PACK)]
         at2 = [keep.tile([P, S], F32, name=f"at2_{t}") for t in range(PACK)]
+        diff = keep.tile([P, PACK, S], F32, name="diff")
 
         def y_out(t):
-            for c in range(4):
-                nc.scalar.activation(y_wins[t][:, c * P : (c + 1) * P], y_banks[c][:, t, :], COPY, scale=gn_sb[:, t : t + 1])
+            for c in range(S // P):
+                nc.scalar.activation(y_win[t][:, block(c)], y_bank[c][:, t, :], COPY, scale=gn_sb[:, t : t + 1])
 
         def y_at1(t):
-            nc.scalar.activation(at1[t][:], y_wins[t][:].indirect(n1_l[:]), COPY)
+            nc.scalar.activation(at1[t][:], y_win[t][:].indirect(n1_l[:]), COPY)
 
         def y_at2(t, half):
-            nc.scalar.activation(at2[t][:, halves[half]], y_wins[t][:].indirect(n2_l[:, half * 16 : (half + 1) * 16]), COPY)
+            entries = n2_l[:, half * (W // PER_COL) : (half + 1) * (W // PER_COL)]
+            nc.scalar.activation(at2[t][:, halves[half]], y_win[t][:].indirect(entries), COPY)
 
         def y_diff(t):
             nc.vector.tensor_tensor(diff[:, t, :], at1[t][:], at2[t][:], ALU.subtract)
 
-        def z_round(c):
-            nc.vector.tensor_tensor(
-                z_grp[:, c * S : (c + 1) * S].rearrange("p (c i t) -> p c t i", i=2, t=PACK),
-                diff[:, :, c * P : (c + 1) * P].rearrange("p t (c i) -> p c t i", i=2),
-                y_banks[c][:].rearrange("p t (c i) -> p c t i", i=2),
-                ALU.mult,
-            )
-
-        s_wins = [keep.tile([P, S], F32, name=f"s_win{t}") for t in range(PACK)]
-        neg_pa = [keep.tile([P, W], F32, name=f"neg_pa{t}") for t in range(PACK)]
-        pb = [keep.tile([P, W], F32, name=f"pb{t}") for t in range(PACK)]
-        rb = [keep.tile([P, W], F32, name=f"rb{t}") for t in range(PACK)]
-        dts = [keep.tile([P, S], F32, name=f"dt{t}") for t in range(PACK)]
-
-        def s_out(t):
-            nc.scalar.activation(s_wins[t][:], s_banks[t][:], COPY, scale=0.0625)
-
-        def s_pair(t):
-            nc.scalar.activation(neg_pa[t][:], s_wins[t][:].indirect(n3_l[:]), COPY, scale=-1.0)
-            nc.scalar.activation(pb[t][:], s_wins[t][:].indirect(n4_l[:]), COPY)
-
-        def put_ra(t):
-            nc.vector.tensor_tensor(dts[t][:].indirect(n3_l[:]), pb[t][:], neg_pa[t][:], ALU.add)
-            nc.vector.scalar_tensor_tensor(rb[t][:], neg_pa[t][:], -0.5, pb[t][:], ALU.mult, ALU.max)
-
-        def put_rb(t):
-            nc.vector.tensor_copy(dts[t][:].indirect(n4_l[:]), rb[t][:])
-
-        def z2_round(t, dt, on_vector):
-            if on_vector:
-                nc.vector.tensor_scalar(z2_planes[:, t, :], dt[:], gk_sb[:, t : t + 1], None, ALU.mult)
-            else:
-                nc.scalar.activation(z2_planes[:, t, :], dt[:], COPY, scale=gk_sb[:, t : t + 1])
-
-        w2_grp = keep.tile([P, N * PACK], BF16, name="w2_grp", align_bytes=64)
-        w3_grp = keep.tile([P, N * PACK], BF16, name="w3_grp", align_bytes=64)
-
-        def w_group(copy, grp, raw, chunks):
-            for c in chunks:
-                interleave(copy, grp[:, c * N : (c + 1) * N], raw[:, :, c * P : (c + 1) * P])
-
-        z_grp = keep.tile([P, S * PACK], BF16, name="z_grp", align_bytes=64)
-        z2_grp = keep.tile([P, S * PACK], BF16, name="z2_grp", align_bytes=64)
         s_out(0)
-        s_pair(0)
-        put_ra(0)
         s_out(1)
-        s_pair(1)
-        put_ra(1)
-        put_rb(0)
-        put_rb(1)
-        z2_round(0, dts[0], True)
-        s_out(2)
+        nc.vector.tensor_scalar(s_win[2][:], s_bank[2][:], 0.0625, None, ALU.mult)
+        for t in (0, 1):
+            s_pairs(t)
+            put_ra_make_rb(t)
+        for t in (0, 1):
+            put_rb(t)
+        for t in (0, 1):
+            nc.vector.tensor_scalar(z2_rows[:, t, :], dt[t][:], gk_sb[:, t : t + 1], None, ALU.mult)
         y_out(0)
         y_out(1)
-        y_at1(0)
-        y_at2(0, 0)
-        s_pair(2)
-        put_ra(2)
-        z2_round(1, dts[1], True)
-        y_at2(0, 1)
-        y_diff(0)
-        put_rb(2)
         s_out(3)
-        y_at1(1)
-        y_out(2)
-        y_at2(1, 0)
-        s_pair(3)
-        put_ra(3)
-        y_at2(1, 1)
-        y_diff(1)
-        put_rb(3)
-        y_out(3)
-        y_at1(2)
-        y_at2(2, 0)
-        y_at2(2, 1)
-        y_diff(2)
-        y_at1(3)
-        y_at2(3, 0)
-        y_at2(3, 1)
-        y_diff(3)
-        def w_tile(t):
-            quantized = []
-            for grp, raw, name in ((w2_grp, w2_raw, "w2"), (w3_grp, w3_raw, "w3")):
-                w_group(nc.scalar.copy, grp, raw, (t,))
-                quantized.append(quantize(grp[:, t * N : (t + 1) * N], f"{name}_{t}"))
-            return quantized
-
-        for c in range(4):
-            z_round(c)
-        z_q = quantize(z_grp[:], "z")
+        for t in (0, 1):
+            y_at1(t)
+            y_at2(t, 0)
+            s_pairs(t + 2)
+            put_ra_make_rb(t + 2)
+            y_at2(t, 1)
+            y_diff(t)
+            put_rb(t + 2)
+            y_out(t + 2)
         for t in (2, 3):
-            z2_round(t, dts[t], False)
-        w_q = [w_tile(0)]
-        interleave(nc.scalar.copy, z2_grp[:, 256 * PACK :], z2_planes[:, :, 256:])
-        interleave(nc.vector.tensor_copy, z2_grp[:, : 256 * PACK], z2_planes[:, :, :256])
+            y_at1(t)
+            y_at2(t, 0)
+            y_at2(t, 1)
+            y_diff(t)
+
+        z_grp = keep.tile([P, S * PACK], BF16, name="z_grp", align_bytes=64)
+        for c in range(S // P):
+            nc.vector.tensor_tensor(
+                z_grp[:, c * P * PACK : (c + 1) * P * PACK].rearrange("p (c i t) -> p c t i", i=2, t=PACK),
+                diff[:, :, block(c)].rearrange("p t (c i) -> p c t i", i=2),
+                y_bank[c][:].rearrange("p t (c i) -> p c t i", i=2),
+                ALU.mult,
+            )
+        z_q = quantize(z_grp[:], "z")
+
+        def w_block(copy, t, tag):
+            grp = keep.tile([P, 2, P * PACK], BF16, name=f"w_grp{t}", tag=tag, align_bytes=64)
+            pair = []
+            for i, raw in enumerate((w2_raw, w3_raw)):
+                interleave(copy, grp[:, i, :], raw[:, :, block(t)])
+                pair.append(quantize(grp[:, i, :], f"w{i + 2}_{t}"))
+            return pair
+
+        for t in (2, 3):
+            nc.scalar.activation(z2_rows[:, t, :], dt[t][:], COPY, scale=gk_sb[:, t : t + 1])
+        w_q = [w_block(nc.scalar.copy, 0, "w_grp0")]
+        z2_grp = keep.tile([P, S * PACK], BF16, name="z2_grp", tag="z2_or_w", align_bytes=64)
+        interleave(nc.scalar.copy, z2_grp[:, Z2_ON_VECTOR * PACK :], z2_rows[:, :, Z2_ON_VECTOR:])
+        interleave(nc.vector.tensor_copy, z2_grp[:, : Z2_ON_VECTOR * PACK], z2_rows[:, :, :Z2_ON_VECTOR])
         z2_q = quantize(z2_grp[:], "z2")
-        w_q.extend(w_tile(t) for t in range(1, 4))
-        w2_q = [pair[0] for pair in w_q]
-        w3_q = [pair[1] for pair in w_q]
+        w_q.extend(w_block(nc.scalar.copy, t, f"w_grp{t}") for t in (1, 2))
+        w_q.append(w_block(nc.vector.tensor_copy, 3, "z2_or_w"))
 
-        h_banks = [psum.tile([P, S], F32, name=f"h_bank{t}", tag=f"sh{t}") for t in range(4)]
-        for t in range(4):
-            product(h_banks[t], w2_q[t], z_q, 0, True, False)
-            product(h_banks[t], w3_q[t], z2_q, 0, False, True)
+        h_bank = [psum.tile([P, S], F32, name=f"h_bank{t}", tag=f"s_or_h{t}") for t in range(PACK)]
+        for t in range(PACK):
+            product(h_bank[t][:], w_q[t][0], block(0), z_q, whole, True, False)
+            product(h_bank[t][:], w_q[t][1], block(0), z2_q, whole, False, True)
 
-        h_win = [keep.tile([P, S], F32, name=f"h_win{t}") for t in range(4)]
-        neg_half = [keep.tile([P, U], F32, name=f"neg_half{t}") for t in range(4)]
-        old = [keep.tile([P, U], F32, name=f"old{t}") for t in range(4)]
-        new = [keep.tile([P, U], F32, name=f"new{t}") for t in range(4)]
-
-        def h_out(t, copy):
-            copy(h_win[t][:], h_banks[t][:])
+        h_win = [keep.tile([P, S], F32, name=f"h_win{t}") for t in range(PACK)]
+        neg_half = [keep.tile([P, U], F32, name=f"neg_half{t}") for t in range(PACK)]
+        at5 = [keep.tile([P, U], F32, name=f"at5_{t}") for t in range(PACK)]
+        least = [keep.tile([P, U], F32, name=f"least{t}") for t in range(PACK)]
 
         def h_half(t):
             nc.scalar.activation(neg_half[t][:], h_win[t][:].indirect(n6_l[:]), COPY, scale=-0.5)
 
-        def h_whole(t):
-            nc.vector.tensor_tensor(old[t][:], h_win[t][:].indirect(n5_l[:]), neg_half[t][:], ALU.add)
-            nc.vector.scalar_tensor_tensor(new[t][:], neg_half[t][:], -1.0, old[t][:], ALU.mult, ALU.min)
+        def ra2_whole(t):
+            nc.vector.tensor_tensor(at5[t][:], h_win[t][:].indirect(n5_l[:]), neg_half[t][:], ALU.add)
+            nc.vector.scalar_tensor_tensor(least[t][:], neg_half[t][:], -1.0, at5[t][:], ALU.mult, ALU.min)
 
-        def h_old_s(t):
-            nc.scalar.activation(old[t][:], h_win[t][:].indirect(n5_l[:]), COPY)
+        def min_only(t):
+            nc.vector.scalar_tensor_tensor(least[t][:], neg_half[t][:], -2.0, at5[t][:], ALU.mult, ALU.min)
 
-        def h_old_v(t):
-            nc.vector.tensor_copy(old[t][:], h_win[t][:].indirect(n5_l[:]))
+        def put_half(t, half):
+            cols = slice(half * (U // 2), (half + 1) * (U // 2))
+            entries = n5_l[:, half * (U // 2 // PER_COL) : (half + 1) * (U // 2 // PER_COL)]
+            nc.vector.tensor_tensor(h_win[t][:].indirect(entries), least[t][:, cols], neg_half[t][:, cols], ALU.add)
 
-        def h_min(t):
-            nc.vector.scalar_tensor_tensor(new[t][:], neg_half[t][:], -2.0, old[t][:], ALU.mult, ALU.min)
-
-        def put_s(t):
-            nc.scalar.activation(h_win[t][:].indirect(n5_l[:]), new[t][:], COPY)
-
-        def put_v(t, part):
-            cols = slice(part * (U // 2), (part + 1) * (U // 2))
-            nc.vector.tensor_tensor(
-                h_win[t][:].indirect(n5_l[:, part * 12 : (part + 1) * 12]), new[t][:, cols], neg_half[t][:, cols], ALU.add
-            )
+        def put_whole(t):
+            nc.scalar.activation(h_win[t][:].indirect(n5_l[:]), least[t][:], COPY)
 
         def store(t):
-            nc.sync.dma_start(out[t * P : (t + 1) * P, :], h_win[t][:])
+            nc.sync.dma_start(out[block(t), :], h_win[t][:])
 
-        h_out(0, nc.scalar.copy)
-        h_out(1, nc.vector.tensor_copy)
-        h_out(2, nc.vector.tensor_copy)
+        nc.scalar.copy(h_win[0][:], h_bank[0][:])
+        nc.vector.tensor_copy(h_win[1][:], h_bank[1][:])
+        nc.vector.tensor_copy(h_win[2][:], h_bank[2][:])
         h_half(0)
-        h_old_v(1)
-        h_whole(0)
+        nc.vector.tensor_copy(at5[1][:], h_win[1][:].indirect(n5_l[:]))
+        ra2_whole(0)
         h_half(1)
-        h_min(1)
+        min_only(1)
         h_half(2)
-        h_out(3, nc.scalar.copy)
-        put_v(1, 0)
-        h_whole(2)
-        put_v(1, 1)
-        store(1)
+        nc.scalar.copy(h_win[3][:], h_bank[3][:])
+        put_half(1, 0)
+        ra2_whole(2)
         h_half(3)
-        h_old_s(3)
-        h_min(3)
-        put_s(0)
+        nc.scalar.activation(at5[3][:], h_win[3][:].indirect(n5_l[:]), COPY)
+        min_only(3)
+        put_whole(0)
         store(0)
-        put_s(2)
+        put_half(3, 0)
+        put_half(1, 1)
+        store(1)
+        put_whole(2)
         store(2)
-        put_v(3, 0)
-        put_v(3, 1)
+        put_half(3, 1)
         store(3)

from contextlib import ExitStack

import concourse.mybir as mybir

F32 = mybir.dt.float32
BF16 = mybir.dt.bfloat16
I32 = mybir.dt.int32
U32 = mybir.dt.uint32
U16 = mybir.dt.uint16
U8 = mybir.dt.uint8
FP8X4 = mybir.dt.float8_e4m3fn_x4
ALU = mybir.AluOpType
COPY = mybir.ActivationFunctionType.Copy

P = 128
PACK = 4
T, G = 1024, 2048
S, H, N = 512, 512, 512
W, U = 256, 384
PER_COL = 16
SPARE = 8
Z2_ON_VECTOR = 128
FLOPS = 4 * 2 * 512 * 512 * 512


def tile_picked_jkeywindliftkmin_none_p_kernel(
    tc, x_words, x_scales, w1, d_words, d_scales, gn, gk, w2, w3, offs, kidx, two, n1, n2, n3, n4, n5, n6, out
):
    nc = tc.nc
    with ExitStack() as ctx:
        keep = ctx.enter_context(tc.tile_pool(name="keep", bufs=1))
        psum = ctx.enter_context(tc.psum_pool(name="psum", bufs=1))
        halves = (slice(0, 256), slice(256, 512))

        def load_list(src, name):
            lst = keep.tile([P, src.shape[1]], U16, name=name)
            nc.sync.dma_start(lst[:], src)
            return lst

        def load_words(src, name):
            table = keep.tile([P, src.shape[2]], U32, name=name)
            nc.sync.dma_start(table[:].bitcast(I32), src[0].rearrange("p n t -> p (n t)").bitcast(I32))
            return table

        def load_gain(src, name):
            gain = keep.tile([P, PACK], F32, name=name)
            nc.sync.dma_start(gain[:], src.rearrange("(p t) o -> p (t o)", t=PACK))
            return gain

        def k_rows(weight):
            return weight.rearrange("(p j) c -> p j c", j=PACK)

        def load_weight(src, name):
            raw = keep.tile([P, PACK, N], F32, name=name)
            nc.sync.dma_start(raw[:], k_rows(src))
            return raw

        def gather(table, lst, dtype, name):
            picked = keep.tile([P, S], dtype, name=name, align_bytes=64)
            nc.vector.tensor_copy(picked[:], table[:].indirect(lst[:]))
            return picked

        def interleave(copy, grouped, rows):
            copy(
                grouped.rearrange("p (c i t) -> p c t i", i=4, t=PACK),
                rows.rearrange("p t (c i) -> p c t i", i=4),
            )

        def quantize(grouped, name):
            cols = grouped.shape[1] // PACK
            codes = keep.tile([P, cols], U32, name=name + "_codes", align_bytes=64)
            plane = keep.tile([P, cols], U8, name=name + "_plane", align_bytes=64)
            nc.vector.quantize_mx(out=codes[:].bitcast(FP8X4), scales=plane[:], in_=grouped)
            return codes, plane

        def product(dst, lhs, lhs_cols, rhs, rhs_cols, start, stop):
            nc.tensor.matmul_mx(
                out=dst,
                lhsT=lhs[0][:, lhs_cols].bitcast(FP8X4),
                lhsT_scale=lhs[1][:, lhs_cols],
                rhs=rhs[0][:, rhs_cols].bitcast(FP8X4),
                rhs_scale=rhs[1][:, rhs_cols],
                start=start,
                stop=stop,
            )

        def block(i):
            return slice(i * P, (i + 1) * P)

        whole = slice(0, S)

        d_bytes = keep.tile([P, G], U8, name="d_bytes")
        x_bytes = keep.tile([P, T], U8, name="x_bytes")
        key_plane = keep.tile([P, H], U8, name="key_plane", align_bytes=64)
        zeros = keep.tile([P, SPARE], F32, name="zeros")
        nc.gpsimd.memset(d_bytes[:].bitcast(I32), 0)
        nc.vector.memset(x_bytes[:].bitcast(I32), 0)
        nc.vector.memset(zeros[:], 0.0)
        nc.vector.memset(key_plane[:].bitcast(I32), 0)

        for q in range(4):
            nc.scalar.dma_start(
                x_bytes[32 * q : 32 * q + 4, :].bitcast(I32), x_scales[0, 4 * q : 4 * q + 4, :].bitcast(I32)
            )
        y_win = [keep.tile([P, S + SPARE], F32, name=f"y_win{t}") for t in range(PACK)]
        for win in y_win:
            nc.scalar.activation(win[:, S:], zeros[:], COPY)
        kidx_l = load_list(kidx, "kidx_l")
        two_l = load_list(two, "two_l")
        nc.sync.dma_start(d_bytes[0:P:8, :].bitcast(I32), d_scales[0].bitcast(I32))
        w1_raw = keep.tile([P, 2, PACK, H // 2], F32, name="w1_raw")
        nc.sync.dma_start(w1_raw[:, 0], k_rows(w1)[:, :, halves[0]])
        x_tab = load_words(x_words, "x_tab")
        d_tab = load_words(d_words, "d_tab")
        nc.sync.dma_start(w1_raw[:, 1], k_rows(w1)[:, :, halves[1]])
        offs_l = load_list(offs, "offs_l")

        key_bytes = gather(d_bytes, kidx_l, U8, "key_bytes")
        key_bytes_dealt = keep.tile([P, H], U8, name="key_bytes_dealt")
        nc.vector.tensor_copy(
            key_bytes_dealt[:].rearrange("p (t m) -> p t m", t=PACK),
            key_bytes[:].rearrange("p (m t) -> p t m", t=PACK),
        )
        for j, queue in enumerate((nc.scalar, nc.scalar, nc.scalar, nc.sync)):
            queue.dma_start(key_plane[j:P:32, :].bitcast(I32), key_bytes_dealt[8 * j : P : 32, :].bitcast(I32))

        n3_l = load_list(n3, "n3_l")
        n4_l = load_list(n4, "n4_l")
        gn_sb = load_gain(gn, "gn_sb")
        n1_l = load_list(n1, "n1_l")
        n2_l = load_list(n2, "n2_l")
        gk_sb = load_gain(gk, "gk_sb")
        w2_raw = load_weight(w2, "w2_raw")
        w3_raw = load_weight(w3, "w3_raw")
        n5_l = load_list(n5, "n5_l")
        n6_l = load_list(n6, "n6_l")

        two_q = (gather(x_tab, two_l, U32, "two_words"), gather(x_bytes, two_l, U8, "two_bytes"))
        key_words = gather(d_tab, kidx_l, U32, "key_words")
        key_dealt = keep.tile([P, H], U32, name="key_dealt", align_bytes=64)
        nc.vector.tensor_copy(
            key_dealt[:].bitcast(I32).rearrange("p (t m) -> p m t", t=PACK),
            key_words[:].bitcast(I32).rearrange("p (m t) -> p m t", t=PACK),
        )
        s_bank = [psum.tile([P, S], F32, name=f"s_bank{t}", tag=f"s_or_h{t}") for t in range(PACK)]
        for t in range(PACK):
            product(s_bank[t][:], (key_dealt, key_plane), block(t), two_q, whole, True, True)

        tok_bytes = gather(x_bytes, offs_l, U8, "tok_bytes")
        tok_words = gather(x_tab, offs_l, U32, "tok_words")
        w1_grp = keep.tile([P, H * PACK], BF16, name="w1_grp", align_bytes=64)
        w1_dealt = w1_grp[:].rearrange("p (t m j) -> p m t j", t=PACK, j=PACK)
        for half in range(2):
            nc.scalar.activation(
                w1_dealt[:, half * (P // 2) : (half + 1) * (P // 2)],
                w1_raw[:, half].rearrange("p j (m t) -> p m t j", t=PACK),
                COPY,
            )
        w1_q = quantize(w1_grp[:], "w1")
        y_bank = [psum.tile([P, PACK, P], F32, name=f"y_bank{c}") for c in range(S // P)]
        for t in range(PACK):
            for c in range(S // P):
                product(y_bank[c][:, t, :], w1_q, block(t), (tok_words, tok_bytes), block(c), True, True)

        s_win = [keep.tile([P, S], F32, name=f"s_win{t}") for t in range(PACK)]
        neg_pa = [keep.tile([P, W], F32, name=f"neg_pa{t}") for t in range(PACK)]
        pb = [keep.tile([P, W], F32, name=f"pb{t}") for t in range(PACK)]
        rb = [keep.tile([P, W], F32, name=f"rb{t}") for t in range(PACK)]
        dt = [keep.tile([P, S], F32, name=f"dt{t}") for t in range(PACK)]
        z2_rows = keep.tile([P, PACK, S], BF16, name="z2_rows")

        def s_out(t):
            nc.scalar.activation(s_win[t][:], s_bank[t][:], COPY, scale=0.0625)

        def s_pairs(t):
            nc.scalar.activation(neg_pa[t][:], s_win[t][:].indirect(n3_l[:]), COPY, scale=-1.0)
            nc.scalar.activation(pb[t][:], s_win[t][:].indirect(n4_l[:]), COPY)

        def put_ra_make_rb(t):
            nc.vector.tensor_tensor(dt[t][:].indirect(n3_l[:]), pb[t][:], neg_pa[t][:], ALU.add)
            nc.vector.scalar_tensor_tensor(rb[t][:], neg_pa[t][:], -0.5, pb[t][:], ALU.mult, ALU.max)

        def put_rb(t):
            nc.vector.tensor_copy(dt[t][:].indirect(n4_l[:]), rb[t][:])

        at1 = [keep.tile([P, S], F32, name=f"at1_{t}") for t in range(PACK)]
        at2 = [keep.tile([P, S], F32, name=f"at2_{t}") for t in range(PACK)]
        diff = keep.tile([P, PACK, S], F32, name="diff")

        def y_out(t):
            for c in range(S // P):
                nc.scalar.activation(y_win[t][:, block(c)], y_bank[c][:, t, :], COPY, scale=gn_sb[:, t : t + 1])

        def y_at1(t):
            nc.scalar.activation(at1[t][:], y_win[t][:].indirect(n1_l[:]), COPY)

        def y_at2(t, half):
            entries = n2_l[:, half * (W // PER_COL) : (half + 1) * (W // PER_COL)]
            nc.scalar.activation(at2[t][:, halves[half]], y_win[t][:].indirect(entries), COPY)

        def y_diff(t):
            nc.vector.tensor_tensor(diff[:, t, :], at1[t][:], at2[t][:], ALU.subtract)

        s_out(0)
        s_out(1)
        nc.vector.tensor_scalar(s_win[2][:], s_bank[2][:], 0.0625, None, ALU.mult)
        for t in (0, 1):
            s_pairs(t)
            put_ra_make_rb(t)
        for t in (0, 1):
            put_rb(t)
        for t in (0, 1):
            nc.vector.tensor_scalar(z2_rows[:, t, :], dt[t][:], gk_sb[:, t : t + 1], None, ALU.mult)
        y_out(0)
        y_out(1)
        s_out(3)
        for t in (0, 1):
            y_at1(t)
            y_at2(t, 0)
            s_pairs(t + 2)
            put_ra_make_rb(t + 2)
            y_at2(t, 1)
            y_diff(t)
            put_rb(t + 2)
            y_out(t + 2)
        for t in (2, 3):
            y_at1(t)
            y_at2(t, 0)
            y_at2(t, 1)
            y_diff(t)

        z_grp = keep.tile([P, S * PACK], BF16, name="z_grp", align_bytes=64)
        for c in range(S // P):
            nc.vector.tensor_tensor(
                z_grp[:, c * P * PACK : (c + 1) * P * PACK].rearrange("p (c i t) -> p c t i", i=2, t=PACK),
                diff[:, :, block(c)].rearrange("p t (c i) -> p c t i", i=2),
                y_bank[c][:].rearrange("p t (c i) -> p c t i", i=2),
                ALU.mult,
            )
        z_q = quantize(z_grp[:], "z")

        def w_block(copy, t, tag):
            grp = keep.tile([P, 2, P * PACK], BF16, name=f"w_grp{t}", tag=tag, align_bytes=64)
            pair = []
            for i, raw in enumerate((w2_raw, w3_raw)):
                interleave(copy, grp[:, i, :], raw[:, :, block(t)])
                pair.append(quantize(grp[:, i, :], f"w{i + 2}_{t}"))
            return pair

        for t in (2, 3):
            nc.scalar.activation(z2_rows[:, t, :], dt[t][:], COPY, scale=gk_sb[:, t : t + 1])
        w_q = [w_block(nc.scalar.copy, 0, "w_grp0")]
        z2_grp = keep.tile([P, S * PACK], BF16, name="z2_grp", tag="z2_or_w", align_bytes=64)
        interleave(nc.scalar.copy, z2_grp[:, Z2_ON_VECTOR * PACK :], z2_rows[:, :, Z2_ON_VECTOR:])
        interleave(nc.vector.tensor_copy, z2_grp[:, : Z2_ON_VECTOR * PACK], z2_rows[:, :, :Z2_ON_VECTOR])
        z2_q = quantize(z2_grp[:], "z2")
        w_q.extend(w_block(nc.scalar.copy, t, f"w_grp{t}") for t in (1, 2))
        w_q.append(w_block(nc.vector.tensor_copy, 3, "z2_or_w"))

        h_bank = [psum.tile([P, S], F32, name=f"h_bank{t}", tag=f"s_or_h{t}") for t in range(PACK)]
        for t in range(PACK):
            product(h_bank[t][:], w_q[t][0], block(0), z_q, whole, True, False)
            product(h_bank[t][:], w_q[t][1], block(0), z2_q, whole, False, True)

        h_win = [keep.tile([P, S], F32, name=f"h_win{t}") for t in range(PACK)]
        neg_half = [keep.tile([P, U], F32, name=f"neg_half{t}") for t in range(PACK)]
        at5 = [keep.tile([P, U], F32, name=f"at5_{t}") for t in range(PACK)]
        least = [keep.tile([P, U], F32, name=f"least{t}") for t in range(PACK)]

        def h_half(t):
            nc.scalar.activation(neg_half[t][:], h_win[t][:].indirect(n6_l[:]), COPY, scale=-0.5)

        def ra2_whole(t):
            nc.vector.tensor_tensor(at5[t][:], h_win[t][:].indirect(n5_l[:]), neg_half[t][:], ALU.add)
            nc.vector.scalar_tensor_tensor(least[t][:], neg_half[t][:], -1.0, at5[t][:], ALU.mult, ALU.min)

        def min_only(t):
            nc.vector.scalar_tensor_tensor(least[t][:], neg_half[t][:], -2.0, at5[t][:], ALU.mult, ALU.min)

        def put_half(t, half):
            cols = slice(half * (U // 2), (half + 1) * (U // 2))
            entries = n5_l[:, half * (U // 2 // PER_COL) : (half + 1) * (U // 2 // PER_COL)]
            nc.vector.tensor_tensor(h_win[t][:].indirect(entries), least[t][:, cols], neg_half[t][:, cols], ALU.add)

        def put_whole(t):
            nc.scalar.activation(h_win[t][:].indirect(n5_l[:]), least[t][:], COPY)

        def store(t):
            nc.sync.dma_start(out[block(t), :], h_win[t][:])

        nc.scalar.copy(h_win[0][:], h_bank[0][:])
        nc.vector.tensor_copy(h_win[1][:], h_bank[1][:])
        nc.vector.tensor_copy(h_win[2][:], h_bank[2][:])
        h_half(0)
        nc.vector.tensor_copy(at5[1][:], h_win[1][:].indirect(n5_l[:]))
        ra2_whole(0)
        h_half(1)
        min_only(1)
        h_half(2)
        nc.scalar.copy(h_win[3][:], h_bank[3][:])
        put_half(1, 0)
        ra2_whole(2)
        h_half(3)
        nc.scalar.activation(at5[3][:], h_win[3][:].indirect(n5_l[:]), COPY)
        min_only(3)
        put_whole(0)
        store(0)
        put_half(3, 0)
        put_half(1, 1)
        store(1)
        put_whole(2)
        store(2)
        put_half(3, 1)
        store(3)
